import numpy as np, ml_dtypes
CORES = [78,86,94,102,110,118]
N = 6
BF = ml_dtypes.bfloat16
def gentries(a):
    return np.ascontiguousarray(a.reshape(8, 16, -1).transpose(0, 2, 1)).reshape(8, -1)
def gtable(e):
    e = np.asarray(e); return np.ascontiguousarray(e.reshape(8, -1, 16).transpose(0, 2, 1)).reshape(128, -1).astype(np.int32)
W, H, L, CAP, RO = 2560, 1024, 128, 192, 4
def pick(t, e):
    return np.take_along_axis(t, e[:, None, :], 2)
def at(x, c):
    return pick(x, c.reshape(8, -1)).reshape(8, 16, 16, -1)
def moved(v, dl):
    return np.clip(v + dl[:, :, None, :], 0, 63)
def spot(u):
    return (((u * u) >> 5) + 37 * u) & (H - 1)
def parts(rng):
    x = rng.integers(0, 64, (N, 8, 16, W)); su = rng.integers(0, W, (N, 8, 16, W)); co = np.argsort(rng.random((N, 8, 16, W)), axis=-1)
    dl = rng.integers(-20, 21, (N, 8, 16, L)); la = rng.integers(0, W, (N, 8, L)); lb = rng.integers(0, W, (N, 8, L))
    wt = rng.integers(0, 256, (N, 8, 16)); th = 110 + 20 * np.argsort(rng.random((N, 8)), axis=-1) + rng.integers(0, 20, (N, 8))
    return x, su, co, dl, la, lb, wt, th
def pack(x, su, co, dl, la, lb, wt, th):
    fl = lambda a, n: np.ascontiguousarray(np.asarray(a).reshape(N, 128, n)).astype(np.float32).astype(BF)
    it = lambda a: np.ascontiguousarray(np.asarray(a).reshape(N, 128, W)).astype(np.int32)
    return {"x0": fl(x, W), "su": it(su), "co": it(co), "dl": fl(dl, L), "la": np.stack([gtable(a) for a in la]), "lb": np.stack([gtable(a) for a in lb]),
            "wt": fl(wt, 1), "th": np.asarray(th).reshape(N, 8, 1).astype(np.int32)}
def put(p, c, v):
    w = np.argmax(p == v[..., None], axis=-1); old = p[..., c].copy()
    np.put_along_axis(p, w[..., None], old[..., None], -1); p[..., c] = v
def two(rng, n):
    c = rng.integers(0, 3, (N, 8, 1, n)); return np.where(c < 2, c, rng.integers(0, 2, (N, 8, 16, n)))
def spots(dl, wt):
    return spot(np.sum(63 * wt[:, :, None] * (dl > 0), axis=1) & 4095)
def setup_inputs(rng):
    return pack(*parts(rng))
def setup_inputs_spread(rng):
    x, su, co, dl, la, lb, wt, th = parts(rng)
    p = np.exp2(rng.integers(-2, 3, (N, 8, 1, W))); x = np.minimum((64 * rng.random((N, 8, 16, W)) ** p).astype(np.int64), 63)
    p = np.exp2(rng.integers(-2, 3, (N, 8, 1, W))); su = np.minimum((W * rng.random((N, 8, 16, W)) ** p).astype(np.int64), W - 1)
    dl = np.rint((2 * rng.random((N, 8, 16, L)) - 1) * rng.choice(np.array([0, 1, 3, 9, 27, 63]), (N, 8, 1, L))).astype(np.int64)
    la = np.minimum((W * rng.random((N, 8, L)) ** 2).astype(np.int64), W - 1); lb = W - 1 - np.minimum((W * rng.random((N, 8, L)) ** 2).astype(np.int64), W - 1)
    wt = np.minimum(np.exp2(8 * rng.random((N, 8, 16))).astype(np.int64), 256) - 1
    th = np.where(rng.random((N, 8)) < 0.5, np.minimum(np.exp2(10 * rng.random((N, 8))).astype(np.int64), 1024) - 1, rng.integers(100, 300, (N, 8)))
    return pack(x, su, co, dl, la, lb, wt, th)
def setup_inputs_ends(rng):
    x, su, co, dl, la, lb, wt, th = parts(rng)
    x = 63 * two(rng, W); su = (W - 1) * two(rng, W); dl = 126 * two(rng, L) - 63
    la = (W - 1) * rng.integers(0, 2, (N, 8, L)); lb = (W - 1) * rng.integers(0, 2, (N, 8, L)); la[:, :, L - 1] = W - 1; lb[:, :, 0] = 0
    wt = 255 * rng.integers(0, 2, (N, 8, 16)); wt[:, 0] = 255 * (np.arange(16) & 1); wt[:, 7] = 255
    th = 1023 * rng.integers(0, 2, (N, 8)); th[:, 0] = 1023; th[:, 1] = 0; th[:, 7] = 0; th[0, 6] = 1023
    z = rng.integers(0, 2, (N, 8, 16)); z[:, :, 0] = 1; z[:, :, 15] = 0
    put(co, 0, (W - 1) * z); put(co, W - 1, (W - 1) * (1 - z))
    dl[:, 7] = np.where(rng.random((N, 1, L)) < 0.5, 63, -63); dl[:, 7, :, 0] = 63; dl[:, 7, :, 1] = -63; dl[:, 7, :, L - 1] = 63
    x[:, 7, :, 0] = 0; x[:, 7, :, W - 1] = 0; x[:, 7, :, spot((16 * 63 * 255) & 4095)] = 0
    x[:, 6, :, 0] = 63; x[:, 6, :, W - 1] = 63; dl[:, 6, :, 0] = -63; dl[:, 6, :, L - 1] = -63
    return pack(x, su, co, dl, la, lb, wt, th)
def setup_inputs_corners(rng):
    x, su, co, dl, la, lb, wt, th = parts(rng); th[:] = 0; dl = 126 * rng.integers(0, 2, (N, 8, 16, L)) - 63
    for r in range(N):
        own = spots(dl[r], wt[r]); come = spots(dl[r - 1], wt[r])
        for i in range(8):
            p = np.unique(own[i]); z = p[:0]
            if i % 2: z = p; p = np.setdiff1d(come[i], z)
            n = int(rng.choice(np.array([0, 1, CAP - 1, CAP, CAP + 1, W - H])))
            if r in (0, N - 1): n = (CAP, CAP, CAP + 1, CAP + 1, CAP - 1, CAP - 1, 0, 1)[i]
            if r == 1 and i in (2, 6): n = W - H
            n = min(n, 16 * len(p), W - H)
            a = np.concatenate([z, p]); s = np.stack([rng.permutation(H)[:len(a)] for k in range(16)])
            c = s[:, len(z):].copy().reshape(-1); c[rng.permutation(len(c))[:n]] = H + rng.permutation(W - H)[:n]
            s[:, len(z):] = c.reshape(16, -1)
            rest = np.ones(W, bool); rest[a] = False
            for k in range(16):
                free = np.ones(W, bool); free[s[k]] = False
                co[r, i, k, a] = s[k]; co[r, i, k, rest] = rng.permutation(np.flatnonzero(free))
    return pack(x, su, co, dl, la, lb, wt, th)
def setup_inputs_crowd(rng):
    x, su, co, dl, la, lb, wt, th = parts(rng)
    dl[:, :2] = 126 * rng.integers(0, 2, (N, 2, 16, L)) - 63
    for i in range(8):
        m = (1, 1, 2, 1, 4, 1, 2, 1)[i]; s = rng.integers(0, m, L); z = int(rng.integers(1, L - 1))
        if i % 2: s[z] = m
        la[:, i] = la[:, i][:, s]; lb[:, i] = lb[:, i][:, s]; dl[:, i] = dl[:, i][:, :, s]
    for r in range(N):
        n = spots(dl[r], wt[r])
        put(co[r, 0], int(n[0, 0]), np.full(16, W - 1)); put(co[r, 1], int(n[1, 0]), np.full(16, H))
        if r % 3 < 2: th[r] = 0
        if r % 3 == 0: dl[r, 5, :, L - 1] = 0; lb[r, 5, L - 1] = la[r, 5, L - 1]
        if r % 3 == 1: th[r, 3] = 1; dl[r, 3, :, L - 1] = 0; lb[r, 3, L - 1] = la[r, 3, L - 1]
    return pack(x, su, co, dl, la, lb, wt, th)
def setup_inputs_ties(rng):
    x, su, co, dl, la, lb, wt, th = parts(rng)
    x = 8 * (x >> 4); x[:, 1::2] = 63 - x[:, 1::2]; dl = 8 * rng.integers(-1, 2, (N, 8, 16, L))
    x[:, 3] = 63; x[:, 3, :7] = 62 + np.minimum(rng.integers(0, 4, (N, 7, W)), 1); dl[:, 3] = -63; dl[2, 3, :, 48:] = 0
    put(co[2, 3], 0, H + np.arange(16)); su[2, 3, :, H:H + 16] = H + ((np.arange(16) + 1) & 15)
    su[:, ::2, :, :W // 2] = su[:, ::2, :1, :W // 2].copy()
    la[:, :, 16:32] = la[:, :, :16].copy(); lb[:, :, 16:32] = lb[:, :, :16].copy(); dl[:, :, :, 16:32] = dl[:, :, :, :16].copy()
    lb[:, :, 32:48] = la[:, :, 32:48].copy(); dl[:, :, :, 32:48] = 0
    for r in range(N):
        dd = np.sum(np.abs(at(x[r], pick(co[r], lb[r])) - moved(at(x[r], pick(co[r], la[r])), dl[r])), axis=1)
        th[r] = np.sort(np.min(dd, axis=1), axis=1)[:, L // 2]; th[r, 4:] += rng.integers(0, 2, 4)
        if r == 2: th[r] = 1023; th[r, 3] = np.min(dd[3, :, :32])
    return pack(x, su, co, dl, la, lb, wt, th)
def check_inputs(d):
    bad = []
    for k, lo, hi in (("x0", 0, 63), ("su", 0, W - 1), ("co", 0, W - 1), ("dl", -63, 63), ("la", 0, W - 1), ("lb", 0, W - 1), ("wt", 0, 255), ("th", 0, 1023)):
        a = np.asarray(d[k]).astype(np.float64)
        if not (np.min(a) >= lo and np.max(a) <= hi): bad.append("range of " + k)
        if np.any(a != np.floor(a)): bad.append("whole numbers of " + k)
    if np.any(np.sort(np.asarray(d["co"]), axis=-1) != np.arange(W)): bad.append("a row of co holds every node once")
    return bad
def reference(x0, su, co, dl, la, lb, wt, th):
    x = x0.astype(np.float32).astype(np.int32).reshape(N, 8, 16, W); s = su.astype(np.int64).reshape(N, 8, 16, W); c = co.astype(np.int64).reshape(N, 8, 16, W)
    sh = dl.astype(np.float32).astype(np.int32).reshape(N, 8, 16, L); w = wt.astype(np.float32).astype(np.int32).reshape(N, 8, 16, 1, 1); lim = th.astype(np.int64).reshape(N, 8, 1)
    a = np.stack([gentries(v) for v in la]).astype(np.int64); b = np.stack([gentries(v) for v in lb]).astype(np.int64)
    flag = np.zeros((N, 8, W), bool); last = np.zeros(N, np.int64)
    for t in range(RO):
        for r in range(N):
            q = (r - t) % N
            d = pick(c[r], a[q]); f = pick(c[r], b[q])
            dist = np.sum(np.abs(at(x[r], f) - moved(at(x[r], d), sh[q])), axis=1)
            k = np.argmin(dist, axis=1)[:, None, :]
            dk = np.take_along_axis(d, k, 1)[:, 0]; fk = np.take_along_axis(f, k, 1)[:, 0]
            same = np.take_along_axis(dist, k, 1)[:, 0] < lim[r] + (last[r] & 63)
            e = moved(at(x[r], pick(s[r], dk)), sh[q])
            n = spot(np.sum(w[r] * e, axis=1).astype(np.int64) & 4095)
            j = np.argmax(np.sum(np.abs(at(x[r], n) - e), axis=1), axis=1)[:, None, :]
            nj = np.take_along_axis(n, j, 1)[:, 0]; ej = np.take_along_axis(e, j[:, None], 2)[:, :, 0]
            for i in range(8):
                lane = np.flatnonzero(~same[i]); place, first = np.unique(nj[i, lane], return_index=True)
                x[r, i][:, place] = ej[i][:, lane[first]]
                flag[r, i, c[r, i][:, place].reshape(-1)] = True; flag[r, i, :H] = False
                v = np.flatnonzero(flag[r, i])[:CAP]
                z = x[r, i][:, s[r, i][:, v]]
                x[r, i][:, v] = (np.max(z, axis=1) + np.min(z, axis=1)) >> 1
                flag[r, i, v] = False
            last[r] = np.sum(~same)
            a[q] = np.where(same, dk, a[q]); b[q] = np.where(same, fk, b[q])
    return {"yx": x.reshape(N, 128, W).astype(np.float32).astype(BF), "ya": np.stack([gtable(a[(r - RO + 1) % N]) for r in range(N)]).astype(np.float32),
            "yb": np.stack([gtable(b[(r - RO + 1) % N]) for r in range(N)]).astype(np.float32)}

@@ -1,0 +1,588 @@
+from concourse.mybir import dt, AluOpType as A, AxisListType, ActivationFunctionType as F
+
+XW = 2752
+CW = 2688
+NA = 64
+EA = 1024
+RO = 4
+FAR1, FAR2 = (2, 3), (2, 3)
+MIX = True
+
+_B, _F, _I, _U = "bfloat16", "float32", "int32", "uint16"
+_S = {
+    "X": (XW, _B), "cot": (CW, _I), "sut": (CW, _I), "dls": (512, _B), "dx0": (2048, _B), "dx1": (2048, _B),
+    "abt": (64, _U), "abo": (64, _U), "lab": (16, _I), "wtc": (1, _B), "thi": (1, _I),
+    "dfk": (256, _U), "f2": (256, _F), "xf": (2048, _B), "xn": (2048, _B), "z": (2048, _B), "z2": (2048, _B), "e1": (2048, _B), "e": (2048, _B),
+    "da": (2048, _B), "db": (2048, _B),
+    "key": (128, _F), "sc": (128, _F), "oh": (128, _F), "pr": (128, _F), "ds": (128, _F), "prf": (128, _F), "fs": (128, _F),
+    "key2": (128, _F), "sc2": (128, _F), "d16": (16, _U), "sj": (128, _U), "ui": (128, _I), "uv": (128, _I), "w1": (128, _F), "w2": (128, _F), "nn": (128, _I),
+    "ni": (128, _I), "n16": (128, _U), "nf": (128, _F), "pay": (128, _F),
+    "k8": (8, _I), "n8": (8, _I), "j8": (8, _I), "nm": (8, _F), "nl": (8, _U), "jf": (8, _F), "jl": (8, _U),
+    "m128": (8, _F), "q": (8, _F), "nb": (8, _F), "cg": (128, _F), "nlx": (128, _F), "esel": (128, _B),
+    "hi": (128, _B), "hs": (128, _B), "lo": (128, _B), "ohl": (4096, _B), "ohh": (6144, _B),
+    "ab1": (1024, _F), "rl": (1024, _F), "los": (8, _F), "lt": (8, _F), "tg": (8, _F), "tg16": (8, _U),
+    "Fl": (96, _B), "Sx": (96, _F), "P2": (96, _B), "Ex": (96, _F), "em": (96, _F), "em2": (96, _F), "tM": (96, _F), "sl16": (16, _U),
+    "Am": (3328, _B), "xr": (192, _B), "xl": (12, _U), "cm": (192, _B), "no16": (12, _U), "s4": (192, _U),
+    "R": (3072, _B), "mx": (3072, _B), "mn": (3072, _B), "sm": (192, _F), "vi": (192, _I),
+    "iv": (12, _F), "vl": (12, _F), "vl16": (12, _U), "g2": (96, _B), "old": (96, _B),
+    "al": (8, _F), "alT": (8, _F), "af": (16, _F), "u8": (16, _F), "abf": (16, _F),
+    "cnt": (1, _F), "ai": (1, _I), "thb": (1, _F), "thv": (1, _F), "th8": (1, _F),
+    "pc": (24, _F), "ci": (160, _I), "cf": (1408, _F), "mf": (1024, _F), "mb": (3024, _B), "rr": (2048, _B), "tmp": (512, _F), "jr": (192, _B),
+    "ks": (1280, _F), "k4": (128, _F),
+}
+SCRATCH = {k: ("sbuf", [128, n], d) for k, (n, d) in _S.items()}
+SCRATCH["a3"] = ("sbuf", [128, 8, 256], _B)
+SCRATCH["b3"] = ("sbuf", [128, 8, 256], _B)
+SCRATCH["t3"] = ("sbuf", [128, 8, 32], _F)
+PSUM = ("pX0", "pX1", "pX2", "pD0", "pD1", "pF", "pM", "pQ")
+for _k in PSUM[:7]:
+    SCRATCH[_k] = ("psum", [128, 512], _F)
+SCRATCH["pQ"] = ("psum", [128, 16, 32], _F)
+LOADS = ["ldla", "ldlb", "ldco", "ldsu", "lddl", "ldx", "ldwt", "ldth"]
+STORES = ["stx0", "stx1", "sta", "stb"]
+SEMAPHORES = ["sV", "sS", "sP", "sG", "loc", "ab1a", "ab2a", "ab3a", "dl1a", "dl2a", "dl3a"] + LOADS + STORES
+CY, PCY, GAT, SCT, WAKE = 0.00104, 0.0006, 1.5, 3.5, 0.06
+
+
+def rank_program(g, core, T, topo):
+    rank = T.rank_of(core)
+    if rank is None:
+        return
+    N = len(T.cores)
+    que = {"V": g.vector, "S": g.scalar, "P": g.tensor, "G": g, "Y": g.sync}
+    cnt = {"V": 0, "S": 0, "P": 0, "G": 0}
+    known = {k: {} for k in que}
+    snap, hist, ops = {}, {}, []
+
+    def v(name, lo=0, hi=None, step=1, p=None):
+        hi = (_S[name][0] if name in _S else 512) if hi is None else hi
+        ps = slice(0, 128) if p is None else slice(p[0], p[1])
+        ap = T[name][ps, lo:hi] if step == 1 else T[name][ps, lo:hi:step]
+        return (ap, [(name, lo, hi, step == 1 and p is None)], -(-(hi - lo) // step))
+
+    def v3(name, w, c0, c1, k0=0, k1=None):
+        k1 = w if k1 is None else k1
+        return (T[name][:, c0:c1, k0:k1], [(name, w * c0, w * c1, k0 == 0 and k1 == w)], (c1 - c0) * (k1 - k0))
+
+    def ind(win, off):
+        return (win[0].indirect(off[0]), win[1] + off[1], 16 * off[2])
+
+    def clash(eng, b, lo, hi, isw, e2, w2, l2, h2):
+        if b in PSUM and e2 != eng:
+            return 2
+        if b in PSUM and e2 == "P":
+            return 1
+        return 2 if (isw or w2) and lo < h2 and l2 < hi else 0
+
+    def need_of(eng, acc):
+        need = {}
+        for (b, lo, hi, _c, isw) in acc:
+            for (e2, c2, w2, l2, h2) in hist.get(b, ()):
+                if need.get(e2, 0) < c2 and clash(eng, b, lo, hi, isw, e2, w2, l2, h2) == 2:
+                    need[e2] = c2
+        return need
+
+    def sem_of(e):
+        return T.sem["s" + e] if e in ("V", "S", "P", "G") else T.sem[e]
+
+    def wait(eng, need):
+        for e2 in sorted(need, key=lambda e: (e != eng, e)):
+            c2 = need[e2]
+            if known[eng].get(e2, 0) < c2:
+                que[eng].wait_ge(sem_of(e2), c2)
+                for k, n in snap.get((e2, c2), {}).items():
+                    if known[eng].get(k, 0) < n:
+                        known[eng][k] = n
+                known[eng][e2] = c2
+
+    def note(e, c, acc):
+        for (b, lo, hi, full, isw) in acc:
+            h = hist.setdefault(b, [])
+            h[:] = [x for x in h if not (((isw and full) or (x[0] == e and x[2] == isw)) and lo <= x[3] and x[4] <= hi)]
+            h.append((e, c, isw, lo, hi))
+
+    def accs(rd, wr):
+        return [a + (False,) for x in rd for a in x[1]] + [a + (True,) for x in wr for a in x[1]]
+
+    def rec(eng, fns, rd, wr, cost, sem=None):
+        ops.append((eng, fns, accs(rd, wr), cost, sem))
+
+    def issue(op):
+        eng, fns, acc, cost, sem = op
+        wait(eng, need_of(eng, acc))
+        if sem is None:
+            for fn in fns:
+                cnt[eng] += 1
+                fn().then_inc(sem_of(eng), 1)
+            s = dict(known[eng])
+            s[eng] = cnt[eng] - 1
+            snap[(eng, cnt[eng])] = s
+            note(eng, cnt[eng], acc)
+        elif sem == "remote":
+            fns[0]()
+        else:
+            fns[0]().then_inc(T.sem[sem], 16)
+            snap[(sem, 16)] = dict(known[eng])
+            note(sem, 16, acc)
+
+    def flush():
+        n = len(ops)
+        succ, npred, h2 = [[] for _ in range(n)], [0] * n, {}
+        for i, (eng, _f, acc, cost, _s) in enumerate(ops):
+            pred = {}
+            for (b, lo, hi, _c, isw) in acc:
+                for (j, e2, w2, l2, hh) in h2.get(b, ()):
+                    c = clash(eng, b, lo, hi, isw, e2, w2, l2, hh)
+                    if c and pred.get(j, 0) < c:
+                        pred[j] = c
+            for (b, lo, hi, full, isw) in acc:
+                h = h2.setdefault(b, [])
+                if isw and full and b not in PSUM:
+                    h[:] = [x for x in h if not (lo <= x[3] and x[4] <= hi)]
+                elif b in PSUM and len(h) > 60:
+                    del h[:-60]
+                h.append((i, eng, isw, lo, hi))
+            for j, c in pred.items():
+                if j != i:
+                    succ[j].append((i, WAKE if c == 2 else 0.0))
+                    npred[i] += 1
+        prio = [0.0] * n
+        for i in range(n - 1, -1, -1):
+            prio[i] = ops[i][3] + max([prio[j] + w for j, w in succ[i]] + [0.0])
+        ready, free = [0.0] * n, {k: 0.0 for k in que}
+        avail = {k: [] for k in que}
+        for i in range(n):
+            if not npred[i]:
+                avail[ops[i][0]].append(i)
+        done = 0
+        while done < n:
+            best = None
+            for e in que:
+                if avail[e]:
+                    t0 = max(free[e], min(ready[i] for i in avail[e]))
+                    i = max((i for i in avail[e] if ready[i] <= t0), key=lambda i: (prio[i], -i))
+                    if best is None or t0 < best[0]:
+                        best = (t0, e, i)
+            t0, e, i = best
+            avail[e].remove(i)
+            free[e] = t0 + (ops[i][3] if ops[i][4] is None else 0.1)
+            for j, w in succ[i]:
+                ready[j] = max(ready[j], t0 + ops[i][3] + w)
+                npred[j] -= 1
+                if not npred[j]:
+                    avail[ops[j][0]].append(j)
+            issue(ops[i])
+            done += 1
+        del ops[:]
+
+    isv = lambda x: isinstance(x, tuple)
+    raw = lambda x: x[0] if isv(x) else x
+    vec, sca, ten = g.vector, g.scalar, g.tensor
+    small = lambda *xs: all(SCRATCH[x[1][0][0]][2] in (_B, _U) for x in xs)
+    isind = lambda x: len(x[1]) > 1
+    inps = lambda x: x[1][0][0] in PSUM
+
+    def vcost(o, a, k=1.0):
+        if isind(a):
+            return 0.05 + GAT * CY * o[2]
+        return max(64, k * o[2]) * CY
+
+    def tt(o, a, b, op):
+        k = 1 if inps(a) or inps(b) else 2
+        rec("V", [lambda: vec.tensor_tensor(o[0], a[0], b[0], op)], [a, b], [o], vcost(o, a, k))
+
+    def ts(o, a, s1, op0, s2=None, op1=None):
+        rd = [a] + [x for x in (s1, s2) if isv(x)]
+        c = vcost(o, a, 0.5 if small(o, a) else 1)
+        if op1 is None:
+            rec("V", [lambda: vec.tensor_scalar(o[0], a[0], raw(s1), None, op0)], rd, [o], c)
+        else:
+            rec("V", [lambda: vec.tensor_scalar(o[0], a[0], raw(s1), raw(s2), op0, op1)], rd, [o], c)
+
+    def cp(o, a, after=()):
+        rec("V", [lambda: vec.tensor_copy(o[0], a[0])], [a] + list(after), [o], vcost(o, a, 0.5 if small(o, a) else 1))
+
+    def scatter(win, off, a):
+        rec("V", [lambda: vec.tensor_copy(win[0].indirect(off[0]), a[0])], [a, off], [win], 0.05 + SCT * CY * a[2])
+
+    def ms(o, c):
+        rec("V", [lambda: vec.memset(o[0], c)], [], [o], max(64, o[2]) * CY)
+
+    def scan(o, a, b, op0, op1):
+        rec("V", [lambda: vec.tensor_tensor_scan(o[0], a[0], b[0], 0.0, op0, op1)], [a, b], [o], vcost(o, b, 0.5 if small(o, a, b) else 1))
+
+    def act(o, a, f=F.Copy, bias=None, scale=None, acc=None):
+        rd = [a] + [x for x in (bias, scale) if isv(x)]
+        kw = {}
+        if bias is not None:
+            kw["bias"] = raw(bias)
+        if scale is not None:
+            kw["scale"] = raw(scale)
+        if acc is not None:
+            kw["accum_out"] = acc[0]
+        rec("S", [lambda: sca.activation(o[0], a[0], f, **kw)], rd, [o] + ([acc] if acc is not None else []), vcost(o, a))
+
+    def mms(o, pairs, start=True, stop=True, f32=False):
+        n = len(pairs)
+        fns = [(lambda l=l, r=r, i=i: ten.matmul(o[0], l[0], r[0], start and i == 0, stop and i == n - 1)) for i, (l, r) in enumerate(pairs)]
+        rd = {}
+        for l, r in pairs:
+            for x in (l, r):
+                for (b, lo, hi, c) in x[1]:
+                    q = rd.get(b, (lo, hi))
+                    rd[b] = (min(lo, q[0]), max(hi, q[1]))
+        cost = sum(max(min(64, l[2]), r[2]) for l, r in pairs) * PCY * (4 if f32 else 1)
+        rec("P", fns, [(None, [(b, lo, hi, False)], 0) for b, (lo, hi) in rd.items()], [o], cost)
+
+    def iota(o, pat, base, cm, **kw):
+        rec("G", [lambda: g.iota(o[0], pat, base, cm, **kw)], [], [o], 0.13 + 2 * CY * o[2])
+
+    def load(eng, name, o, src, after=()):
+        rec(eng, [lambda: que[eng].dma_start(o[0], src[:])], list(after), [o], 3.0 + o[2] * 0.0015, name)
+
+    def store(name, dst, a):
+        rec("Y", [lambda: g.sync.dma_start(dst, a[0])], [a], [], 3.0, name)
+
+    locs = [0]
+    trip = lambda s: (None, [("~" + s, 0, 1, True)], 0)
+
+    def remote(dst, name, lo, hi, a, rsem):
+        rid, pid = topo.addr(dst)[:2]
+        en = topo.engines(core, dst)[:4]
+        locs[0] += len(en)
+        rec("G", [lambda: g.remote_dma(T[name][:, lo:hi], a[0], T.sem[rsem], T.sem.loc, pid, rid, sum(1 << x for x in en))], [a], [trip(rsem)], 14.0, "remote")
+        return len(en)
+
+    lab = v("lab")
+    load("Y", "ldla", v("lab", 0, 8), T.la)
+    load("Y", "ldlb", v("lab", 8, 16), T.lb)
+    load("Y", "ldco", v("cot", 0, 2560), T.co)
+    load("S", "lddl", v("dls", 0, 128), T.dl)
+    load("S", "ldx", v("X", 0, 2560), T.x0)
+    load("Y", "ldth", (T.thi[0:8, 0:1], [("thi", 0, 1, True)], 1), T.th)
+    load("Y", "ldwt", v("wtc"), T.wt)
+    load("Y", "ldsu", v("sut", 0, 2560), T.su, [v("cot", 0, 2560)])
+    landed = {}
+    for s in range(1, RO):
+        dst = T.cores[(rank + s) % N]
+        k = remote(dst, "dls", 128 * s, 128 * s + 128, v("dls", 0, 128), "dl%da" % s)
+        landed["dl%da" % s], landed["ab%da" % s] = k, k
+        note("dl%da" % s, k, [("dls", 128 * s, 128 * s + 128, True, True)])
+        note("ab%da" % s, k, [("abt", 16 * s, 16 * s + 16, True, True)])
+
+    def spread(t):
+        for k in range(16):
+            act(v("dx%d" % (t % 2), k, 2048, 16), v("dls", 128 * t, 128 * t + 128))
+
+    spread(0)
+
+    iota(v("ci", 0, 128), [[1, 128]], 0, 0)
+    iota(v("ci", 128, 129), [[0, 1]], 0, 1)
+    iota(v("tmp"), [[1, 512]], 0, 0, allow_small_or_imprecise_dtypes=True)
+    col = lambda n: v("tmp", 0, n)
+    cp(v("abt", 0, 16), lab)
+    ms(v("cot", 2560, CW), 0)
+    ms(v("sut", 2560, CW), 0)
+    P = lambda i: v("pc", i, i + 1)
+    cp(P(0), v("ci", 128, 129))
+    for d, s1, op in ((129, 4, A.arith_shift_right), (130, 15, A.bitwise_and), (131, 5, A.arith_shift_right), (132, 16, A.bitwise_and)):
+        ts(v("ci", d, d + 1), v("ci", 128, 129), s1, op)
+    for d, s in ((1, 129), (2, 130), (3, 131)):
+        cp(P(d), v("ci", s, s + 1))
+    ts(P(5), v("ci", 132, 133), 1.0 / 16, A.mult)
+    ts(P(4), P(5), -1.0, A.mult, 1.0, A.add)
+    ts(P(6), P(3), 4.0, A.add)
+    ts(P(8), P(2), 0.0, A.is_equal)
+    tt(P(9), P(0), P(2), A.subtract)
+    ts(P(10), P(9), 15.0, A.add)
+    MB = {"B1": 0, "B16k": 144, "W": 288, "FR": 432, "FR16": 576, "I": 720, "nI": 848, "U": 976}
+    for i, k in enumerate(("T", "O", "C")):
+        for b in range(4):
+            MB[k + str(b)] = 1488 + 128 * (4 * i + b)
+    mb = lambda k, n=128: v("mb", MB[k], MB[k] + n)
+    slide = lambda k, m: v("mb", MB[k] + 15 - m, MB[k] + 143 - m)
+    CF, at = {}, [0]
+
+    def cf(k, n):
+        CF[k] = (at[0], n)
+        at[0] += n
+        return v("cf", CF[k][0], CF[k][0] + n)
+
+    C = lambda k, lo=0, hi=None: v("cf", CF[k][0] + lo, CF[k][0] + (CF[k][1] if hi is None else hi))
+    MF = {"I": 0, "BO": 128, "ON": 256, "E8": 384, "SW00": 512, "SW01": 640, "SW10": 768, "SW11": 896}
+    mf = lambda k: v("mf", MF[k], MF[k] + 128)
+    ts(mb("B1", 144), col(144), P(10), A.is_equal)
+    ts(v("ci", 0, 128), v("ci", 0, 128), 15, A.bitwise_and)
+    cp(cf("kc", 128), v("ci", 0, 128))
+    ts(cf("k16", 128), C("kc"), 1.0 / 16, A.mult)
+    ts(cf("R1", 128), C("kc"), 0.0, A.is_equal, 32768.0, A.mult)
+    ts(cf("R3", 128), C("kc"), 0.0, A.is_gt)
+    ts(mf("I"), col(128), P(0), A.is_equal)
+    for cpx in range(2):
+        for gp in range(2):
+            ts(P(11 + 2 * cpx + gp), P(0), 16.0 * (gp - cpx), A.add)
+            ts(mf("SW%d%d" % (cpx, gp)), col(128), P(11 + 2 * cpx + gp), A.is_equal, P(4 + cpx), A.mult)
+    cp(mb("I"), mf("I"))
+    ts(mb("nI"), mf("I"), -1.0, A.mult)
+    ts(mb("W", 144), mb("B1", 144), v("wtc"), A.mult)
+    tt(v("k4"), col(128), C("kc"), A.subtract)
+    ts(cf("c4", 128), v("k4"), 1.0 / 16, A.mult)
+    ts(mf("E8"), C("c4"), P(0), A.is_equal)
+    th8 = v("th8", 0, 1, 1, (0, 8))
+    cp(th8, v("thi", 0, 1, 1, (0, 8)))
+    mms(v("pM", 0, 1), [(v("mf", MF["E8"], MF["E8"] + 128, 1, (0, 8)), th8)], f32=True)
+    cp(v("thb"), v("pM", 0, 1))
+    cp(v("thv"), v("thb"))
+    ts(cf("R2", 128), C("kc"), 0.0, A.is_gt, 16777216.0, A.mult)
+    ts(cf("pc2", 128), C("kc"), -1024.0, A.mult, 15360.0, A.add)
+    ts(mb("B16k", 144), mb("B1", 144), 16384.0, A.mult)
+    ts(mf("BO"), C("c4"), P(1), A.is_equal)
+    ms(mf("ON"), 1.0)
+    ts(cf("M16", 96), C("kc", 0, 96), P(2), A.is_equal)
+    ts(cf("lf", 8), col(8), 16.0, A.mult, P(2), A.add)
+    ts(cf("cT", 8), C("lf"), 2560.0, A.add)
+    ts(cf("c15", 8), C("lf"), 16.0, A.mult, 15.0, A.add)
+    ts(cf("hl", 8), C("lf"), 0.5, A.mult)
+    ts(cf("c2", 8), C("lf"), -0.5, A.mult, 0.5, A.add)
+    ts(mb("FR", 144), mb("B1", 144), P(8), A.mult)
+    ts(mb("FR16", 144), mb("FR", 144), 16.0, A.mult)
+    ts(v("ks", 0, 128), C("kc"), P(2), A.is_equal)
+    ts(v("ks", 128, 256), C("kc"), P(2), A.is_lt, -1.0, A.mult)
+    for Q in range(2):
+        for b in range(2):
+            i = str(2 * Q + b)
+            ts(mb("O" + i), C("c4"), P(6 if Q else 3), A.is_equal, P(4 + b), A.mult)
+            tt(mb("C" + i), mb("O" + i), v("ks", 0, 128), A.mult)
+            tt(mb("T" + i), mb("O" + i), v("ks", 128, 256), A.mult)
+    ts(P(16), P(1), 64.0, A.mult, P(2), A.add)
+    ts(P(17), P(16), 48.0, A.add)
+    ts(v("ks", 256, 768), col(512), P(16), A.is_equal)
+    ts(v("ks", 768, 1280), col(512), P(17), A.is_equal)
+    tt(mb("U", 512), v("ks", 256, 768), v("ks", 768, 1280), A.add)
+    ts(v("k4", 0, 96), col(96), 1600.0, A.add)
+    tt(cf("cxM", 96), v("k4", 0, 96), C("M16"), A.mult)
+    cp(v("jr"), col(192))
+    ms(cf("one", 96), 1.0)
+    ts(cf("jl", 12), col(12), 16.0, A.mult, P(2), A.add)
+    ts(cf("jT", 12), C("jl"), 1536.0, A.add)
+    for i in range(8):
+        ts(v("rr", 128 * i, 128 * i + 128), C("kc"), 0.0, A.is_gt, 64.0, A.mult)
+        ts(v("rr", 1024 + 128 * i, 1152 + 128 * i), C("kc"), 0.0, A.is_equal, 64.0, A.mult)
+
+    ADD, SUB, MUL, MAX, MIN = A.add, A.subtract, A.mult, A.max, A.min
+    X, cot, sut = v("X", 0, 2560), v("cot"), v("sut")
+    PART = {0: (0, NA), 1: (NA, 128)}
+    PU = {1: "pF", 0: "pM"}
+
+    def turn(src, nblk):
+        if MIX:
+            o, i = v3("t3", 32, 0, nblk), v(src, 0, 32 * nblk)
+            rec("V", [lambda: vec.transpose(o[0], i[0])], [i], [o], 32 * nblk * CY)
+            return
+        for a in range(nblk):
+            o = (T.t3[:, a, :], [("t3", 32 * a, 32 * a + 32, True)], 32)
+            i = v(src, 32 * a, 32 * a + 32)
+            rec("V", [lambda o=o, i=i: vec.transpose(o[0], i[0])], [i], [o], 64 * CY)
+
+    def swap(nblk):
+        for cpx in range(2):
+            mms(v3("pQ", 32, 0, nblk, 16 * cpx, 16 * cpx + 16),
+                [(mf("SW%d%d" % (cpx, gp)), v3("t3", 32, 0, nblk, 16 * gp, 16 * gp + 16)) for gp in range(2)], f32=True)
+
+    def with_q(o, lo, hi, q0, b, op):
+        if MIX:
+            tt(v(o, lo, hi), v3("pQ", 32, (q0 + lo) // 32, (q0 + hi) // 32), b(lo, hi), op)
+            return
+        for c in range(lo // 16, hi // 16):
+            x = q0 // 16 + c
+            q = (T.pQ[:, x // 2, 16 * (x % 2):16 * (x % 2) + 16], [("pQ", 16 * x, 16 * x + 16, False)], 16)
+            tt(v(o, 16 * c, 16 * c + 16), q, b(16 * c, 16 * c + 16), op)
+
+    def distance(pd, w, buf, part):
+        c0 = 4 * part
+        mms(v(pd, 0, NA), [(slide(w, m), v3(buf, 256, c0, c0 + 4, 16 * m, 16 * m + 16)) for m in range(16)])
+
+    BANK = ("pX2", "pM", "pX0", "pX1")
+
+    def far(xb, eb, ab, lists, l0, quarters):
+        for i in quarters:
+            act(v(xb, 512 * i, 512 * i + 512), ind(X, v(lists, l0 + 32 * i, l0 + 32 * i + 32)))
+        for i in quarters:
+            p = v(BANK[i])
+            mms(p, [(mb("I"), v(xb, 512 * i, 512 * i + 512)), (mb("nI"), v(eb, 512 * i, 512 * i + 512))])
+            act(v3(ab, 256, 2 * i, 2 * i + 2), p, F.Abs)
+
+    def near(eb, ab, db, lists, l0, quarters):
+        for i in quarters:
+            tt(v(db, 512 * i, 512 * i + 512), ind(X, v(lists, l0 + 32 * i, l0 + 32 * i + 32)), v(eb, 512 * i, 512 * i + 512), SUB)
+            act(v3(ab, 256, 2 * i, 2 * i + 2), v(db, 512 * i, 512 * i + 512), F.Abs)
+
+    def clip(o, z, part):
+        ts(v(o, EA * part, EA * part + EA), v(z, EA * part, EA * part + EA), 0.0, MAX, 63.0, MIN)
+
+    for t in range(RO):
+        dx = "dx%d" % (t % 2)
+        last = t == RO - 1
+        ab, here = v("abt", 16 * t, 16 * t + 16), [trip("ab%da" % t)]
+        cp(v("dfk"), ind(cot, ab), here)
+        for part in (1, 0):
+            lo, hi = PART[part]
+            tt(v("z", 16 * lo, 16 * hi), ind(X, v("dfk", lo, hi)), v(dx, 16 * lo, 16 * hi), ADD)
+            clip("e1", "z", part)
+        cp(v("f2"), v("dfk"))
+        turn("f2", 8)
+        far("xf", "e1", "a3", "dfk", 128, FAR1)
+        near("e1", "a3", "da", "dfk", 128, [i for i in (3, 2, 0, 1) if i not in FAR1])
+        swap(8)
+        distance("pD1", "B1", "a3", 1)
+        distance("pD0", "B1", "a3", 0)
+
+        for part in (1, 0):
+            lo, hi = PART[part]
+            tt(v("key", lo, hi), v("pD%d" % part, 0, NA), C("k16", lo, hi), ADD)
+            scan(v("sc", lo, hi), C("R1", lo, hi), v("key", lo, hi), MAX, MIN)
+            for c in range(lo // 16, hi // 16):
+                ts(v("oh", 16 * c, 16 * c + 16), v("key", 16 * c, 16 * c + 16), v("sc", 16 * c + 15, 16 * c + 16), A.is_equal)
+            with_q("pr", lo, hi, 0, lambda a, b: v("oh", a, b), MUL)
+            scan(v("ds", lo, hi), C("R3", lo, hi), v("pr", lo, hi), MUL, ADD)
+            cp(v("d16", 4 * part, 4 * part + 4), v("ds", lo + 15, hi, 16))
+            cp(v("sj", lo, hi), ind(sut, v("d16", 4 * part, 4 * part + 4)))
+            tt(v("z2", 16 * lo, 16 * hi), ind(X, v("sj", lo, hi)), v(dx, 16 * lo, 16 * hi), ADD)
+            clip("e", "z2", part)
+            mms(v(PU[part], 0, NA), [(slide("W", j), v("e", 16 * lo + j, 16 * hi, 16)) for j in range(16)])
+            r = lambda k: v(k, lo, hi)
+            cp(r("ui"), v(PU[part], 0, NA))
+            ts(r("uv"), r("ui"), 4095, A.bitwise_and)
+            ts(r("w1"), r("uv"), -2048.0, ADD)
+            ts(r("w2"), r("uv"), 3232.0, ADD)
+            tt(r("nn"), r("w1"), r("w2"), MUL)
+            ts(r("ni"), r("nn"), 5, A.arith_shift_right, 1023, A.bitwise_and)
+            cp(r("n16"), r("ni"))
+            cp(r("nf"), r("ni"))
+        with_q("prf", 0, 128, 128, lambda a, b: v("oh", a, b), MUL)
+        scan(v("fs"), C("R3"), v("prf"), MUL, ADD)
+        ts(v("al"), v("sc", 15, 128, 16), v("thv"), A.is_lt)
+        tt(v("alT"), v("al"), C("cT"), MUL)
+        far("xn", "e", "b3", "n16", 0, FAR2)
+        near("e", "b3", "db", "n16", 0, [i for i in (3, 2, 0, 1) if i not in FAR2])
+        turn("nf", 4)
+        swap(4)
+        distance("pD1", "B16k", "b3", 1)
+        distance("pD0", "B16k", "b3", 0)
+        with_q("pay", 0, 128, 0, lambda a, b: C("pc2", a, b), ADD)
+        for part in (1, 0):
+            lo, hi = PART[part]
+            tt(v("key2", lo, hi), v("pD%d" % part, 0, NA), v("pay", lo, hi), ADD)
+            scan(v("sc2", lo, hi), C("R2", lo, hi), v("key2", lo, hi), MIN, MAX)
+        cp(v("af"), ab, here)
+        tt(v("u8", 0, 8), v("ds", 15, 128, 16), v("af", 0, 8), SUB)
+        tt(v("u8", 8, 16), v("fs", 15, 128, 16), v("af", 8, 16), SUB)
+        for h in (0, 8):
+            tt(v("u8", h, h + 8), v("u8", h, h + 8), v("al"), MUL)
+        tt(v("abf"), v("u8"), v("af"), ADD)
+        if not last:
+            cp(v("abo", 16 * t, 16 * t + 16), v("abf"))
+            remote(T.cores[(rank + 1) % N], "abt", 16 * t + 16, 16 * t + 32, v("abo", 16 * t, 16 * t + 16), "ab%da" % (t + 1))
+            rec("V", [lambda: vec.tensor_reduce(T.cnt[:, 0:1], T.al[:, 0:8], AxisListType.X, ADD)], [v("al")], [v("cnt")], 64 * CY)
+        else:
+            store("sta", T.ya[:], v("abf", 0, 8))
+            store("stb", T.yb[:], v("abf", 8, 16))
+        cp(v("k8"), v("sc2", 15, 128, 16))
+        ts(v("n8"), v("k8"), 1023, A.bitwise_and)
+        ts(v("j8"), v("k8"), 10, A.arith_shift_right, 15, A.bitwise_and)
+        tt(v("nm"), v("n8"), v("alT"), MAX)
+        cp(v("nl"), v("nm"))
+        cp(v("cg"), ind(cot, v("nl")))
+        rec("P", [lambda: ten.transpose(T.pX2[:, 0:128], T.cg[:, 0:128], mf("I")[0])], [v("cg"), mf("I")], [v("pX2", 0, 128)], 512 * PCY)
+        ts(v("m128"), v("nm"), 128.0, MUL)
+        tt(v("q"), v("m128"), C("lf"), ADD)
+        tt(v("nb"), C("c2"), v("m128"), SUB)
+        for c in range(8):
+            act(v("nlx", 16 * c, 16 * c + 16), C("M16", 0, 16), F.Copy, scale=v("q", c, c + 1))
+        mms(v("pM", 0, 128), [(mf("BO"), v("nlx"))], f32=True)
+        for c in range(8):
+            act(v("ab1", 128 * c, 128 * c + 16 * c + 16), v("pM", 0, 16 * c + 16), F.Abs, bias=v("nb", c, c + 1))
+        for c in range(8):
+            act(v("rl", 128 * c, 128 * c + 16 * c + 16), v("ab1", 128 * c, 128 * c + 16 * c + 16), F.Relu, bias=C("hl", c, c + 1), scale=-1.0, acc=v("los", c, c + 1))
+        ts(v("lt"), v("los"), 0.0, A.is_gt)
+        tt(v("lt"), v("lt"), C("cT"), MUL)
+        tt(v("tg"), v("lt"), v("nm"), MAX)
+        cp(v("tg16"), v("tg"))
+        tt(v("jf"), C("c15"), v("j8"), SUB)
+        cp(v("jl"), v("jf"))
+        cp(v("esel"), ind(v("e"), v("jl")))
+        scatter(v("X"), v("tg16"), v("esel"))
+        if last:
+            store("stx0", T.yx[:, 0:1024], v("X", 0, 1024))
+        ts(v("hi"), v("pX2", 0, 128), 1.0 / 32, MUL, 128.0 - 31.0 / 64, ADD)
+        ts(v("hs"), v("hi"), -32.0, MUL, 4096.0, ADD)
+        tt(v("lo"), v("pX2", 0, 128), v("hs"), ADD)
+        for h in range(48):
+            ts(v("ohh", 128 * h, 128 * h + 128), v("hi"), 160.0 + h, A.is_equal)
+        for h in range(32):
+            ts(v("ohl", 128 * h, 128 * h + 128), v("lo"), float(h), A.is_equal)
+        for gi in range(8):
+            Q, q4 = divmod(gi, 4)
+            pairs = [(v("ohl", 16 * gi + k, 4096, 128), v("ohh", 16 * gi + k, 6144, 128)) for k in range(16)]
+            if t:
+                pairs += [(v("mb", MB["U"] + 64 * gi + 32 * b, MB["U"] + 64 * gi + 32 * b + 32), v("old", b, 96, 2)) for b in range(2)]
+            mms(v("pF", 48 * Q, 48 * Q + 48, 1, (32 * q4, 32 * q4 + 32)), pairs)
+        if not last:
+            spread(t + 1)
+            mms(v("pM", 0, 1), [(mf("ON"), v("cnt"))], f32=True)
+            ts(v("ai"), v("pM", 0, 1), -1.0, MUL, 1024.0, ADD)
+            ts(v("ai"), v("ai"), 63, A.bitwise_and)
+            tt(v("thv"), v("thb"), v("ai"), ADD)
+        ts(v("Fl"), v("pF", 0, 96), 0.0, A.is_gt)
+        for mi, bank in (("O", "pX0"), ("T", "pX1")) + ((("C", "pD0"),) if not last else ()):
+            for b in range(2):
+                mms(v(bank, b, 96, 2), [(mb(mi + str(2 * Q + b)), v("Fl", 48 * Q, 48 * Q + 48)) for Q in range(2)])
+        tot = v("pX0", 0, 96)
+        scan(v("Sx"), C("one"), tot, MUL, ADD)
+        ts(v("em"), tot, 0.0, A.is_equal)
+        tt(v("tM"), tot, C("M16"), MUL)
+        tt(v("em"), v("em"), C("cxM"), MUL)
+        tt(v("em2"), v("em"), v("tM"), SUB)
+        tt(v("Ex"), v("Sx"), C("M16"), MUL)
+        tt(v("Ex"), v("Ex"), v("em2"), ADD)
+        scan(v("em"), C("R3", 0, 96), v("Ex"), MUL, ADD)
+        cp(v("sl16", 0, 6), v("em", 15, 96, 16))
+        tt(v("P2"), v("Sx"), v("pX1", 0, 96), ADD)
+        ms(v("Am", 0, 192), 0.0)
+        scatter(v("Am"), v("sl16", 0, 6), v("jr", 0, 96))
+        scan(v("xr"), v("Am", 0, 192), v("Am", 0, 192), MAX, MAX)
+        mms(v("pX2", 0, 12), [(slide("FR", m), v("xr", m, 192, 16)) for m in range(16)])
+        cp(v("xl"), v("pX2", 0, 12))
+        mms(v("pD1", 0, 12), [(slide("FR16", m), v("xr", m, 192, 16)) for m in range(16)], True, False)
+        tt(v("cm"), ind(v("P2"), v("xl")), v("jr"), A.is_le)
+        mms(v("pD1", 0, 12), [(slide("B1", m), v("cm", m, 192, 16)) for m in range(16)], False, True)
+        ts(v("no16"), v("pD1", 0, 12), 1024.0, ADD)
+        cp(v("s4"), ind(sut, v("no16")))
+        for c in (1, 2):
+            act(v("R", 1024 * c, 1024 * c + 1024), ind(X, v("s4", 64 * c, 64 * c + 64)))
+        cp(v("R", 0, 1024), ind(X, v("s4", 0, 64)))
+        ts(v("iv"), C("jl"), v("Sx", 95, 96), A.is_ge)
+        tt(v("iv"), v("iv"), C("jT"), MUL)
+        tt(v("vl"), v("pD1", 0, 12), v("iv"), MAX)
+        cp(v("vl16"), v("vl"))
+        if not last:
+            ts(v("g2"), v("P2"), 192.0, A.is_gt)
+            tt(v("old"), v("pD0", 0, 96), v("g2"), MUL)
+        for c in range(3):
+            r = v("R", 1024 * c, 1024 * c + 1024)
+            scan(v("mx", 1024 * c, 1024 * c + 1024), v("rr", 0, 1024), r, MIN, MAX)
+            scan(v("mn", 1024 * c, 1024 * c + 1024), v("rr", 1024, 2048), r, MAX, MIN)
+            tt(v("sm", 64 * c, 64 * c + 64), v("mx", 1024 * c + 15, 1024 * c + 1024, 16), v("mn", 1024 * c + 15, 1024 * c + 1024, 16), ADD)
+            ts(v("vi", 64 * c, 64 * c + 64), v("sm", 64 * c, 64 * c + 64), 0.5, MUL, -0.25, ADD)
+        scatter(v("X", 1024, XW), v("vl16"), v("vi"))
+    store("stx1", T.yx[:, 1024:2560], v("X", 1024, 2560))
+    flush()
+
+    for e in ("V", "S", "P", "G"):
+        wait("G", {e: cnt[e]})
+    for k in LOADS:
+        wait("G", {k: 16})
+    for k in STORES:
+        g.sync.wait_ge(T.sem[k], 16)
+    g.wait_ge(T.sem.loc, locs[0])
+    wait("G", landed)

@@ -3,10 +3,11 @@ from concourse.mybir import dt, AluOpType as A, AxisListType, ActivationFunction
 XW = 2752
 CW = 2688
 NA = 64
-EA = 1024
 RO = 4
-FAR1, FAR2 = (2, 3), (2, 3)
-MIX = True
+ZS1, ZS2 = (1,), (1,)
+FAR1, FAR2 = (2, 3), (2,)
+NS = 14
+RC = (48, 80, 64)
 
 _B, _F, _I, _U = "bfloat16", "float32", "int32", "uint16"
 _S = {
@@ -19,15 +20,15 @@ _S = {
     "ni": (128, _I), "n16": (128, _U), "nf": (128, _F), "pay": (128, _F),
     "k8": (8, _I), "n8": (8, _I), "j8": (8, _I), "nm": (8, _F), "nl": (8, _U), "jf": (8, _F), "jl": (8, _U),
     "m128": (8, _F), "q": (8, _F), "nb": (8, _F), "cg": (128, _F), "nlx": (128, _F), "esel": (128, _B),
-    "hi": (128, _B), "hs": (128, _B), "lo": (128, _B), "ohl": (4096, _B), "ohh": (6144, _B),
+    "hi": (128, _B), "hs": (128, _B), "lo": (128, _B), "sh": (2048, _B), "ohl": (4096, _B), "ohh": (6144, _B),
     "ab1": (1024, _F), "rl": (1024, _F), "los": (8, _F), "lt": (8, _F), "tg": (8, _F), "tg16": (8, _U),
-    "Fl": (96, _B), "Sx": (96, _F), "P2": (96, _B), "Ex": (96, _F), "em": (96, _F), "em2": (96, _F), "tM": (96, _F), "sl16": (16, _U),
-    "Am": (3328, _B), "xr": (192, _B), "xl": (12, _U), "cm": (192, _B), "no16": (12, _U), "s4": (192, _U),
+    "Fl": (96, _B), "Sx": (96, _F), "P2": (112, _B), "sg": (1152, _B), "xa": (12, _F), "xb": (12, _B), "xl": (12, _U),
+    "cm": (192, _B), "no16": (12, _U), "s4": (192, _U),
     "R": (3072, _B), "mx": (3072, _B), "mn": (3072, _B), "sm": (192, _F), "vi": (192, _I),
     "iv": (12, _F), "vl": (12, _F), "vl16": (12, _U), "g2": (96, _B), "old": (96, _B),
     "al": (8, _F), "alT": (8, _F), "af": (16, _F), "u8": (16, _F), "abf": (16, _F),
     "cnt": (1, _F), "ai": (1, _I), "thb": (1, _F), "thv": (1, _F), "th8": (1, _F),
-    "pc": (24, _F), "ci": (160, _I), "cf": (1408, _F), "mf": (1024, _F), "mb": (3024, _B), "rr": (2048, _B), "tmp": (512, _F), "jr": (192, _B),
+    "pc": (24, _F), "ci": (160, _I), "cf": (1408, _F), "mf": (1024, _F), "mb": (3024, _B), "rr": (3072, _B), "tmp": (512, _F), "jr": (192, _B),
     "ks": (1280, _F), "k4": (128, _F),
 }
 SCRATCH = {k: ("sbuf", [128, n], d) for k, (n, d) in _S.items()}
@@ -38,10 +39,11 @@ PSUM = ("pX0", "pX1", "pX2", "pD0", "pD1", "pF", "pM", "pQ")
 for _k in PSUM[:7]:
     SCRATCH[_k] = ("psum", [128, 512], _F)
 SCRATCH["pQ"] = ("psum", [128, 16, 32], _F)
+BANK = ("pX2", "pM", "pX0", "pX1")
 LOADS = ["ldla", "ldlb", "ldco", "ldsu", "lddl", "ldx", "ldwt", "ldth"]
 STORES = ["stx0", "stx1", "sta", "stb"]
 SEMAPHORES = ["sV", "sS", "sP", "sG", "loc", "ab1a", "ab2a", "ab3a", "dl1a", "dl2a", "dl3a"] + LOADS + STORES
-CY, PCY, GAT, SCT, WAKE = 0.00104, 0.0006, 1.5, 3.5, 0.06
+CY, PCY, GAT, SCT, WAKE = 0.00104, 0.0007, 1.5, 3.5, 0.08
 
 
 def rank_program(g, core, T, topo):
@@ -292,10 +294,9 @@ def rank_program(g, core, T, topo):
     ts(P(5), v("ci", 132, 133), 1.0 / 16, A.mult)
     ts(P(4), P(5), -1.0, A.mult, 1.0, A.add)
     ts(P(6), P(3), 4.0, A.add)
-    ts(P(8), P(2), 0.0, A.is_equal)
     tt(P(9), P(0), P(2), A.subtract)
     ts(P(10), P(9), 15.0, A.add)
-    MB = {"B1": 0, "B16k": 144, "W": 288, "FR": 432, "FR16": 576, "I": 720, "nI": 848, "U": 976}
+    MB = {"B1": 0, "B16k": 144, "W": 288, "I16": 432, "I": 720, "nI": 848, "U": 976}
     for i, k in enumerate(("T", "O", "C")):
         for b in range(4):
             MB[k + str(b)] = 1488 + 128 * (4 * i + b)
@@ -338,14 +339,13 @@ def rank_program(g, core, T, topo):
     ts(mb("B16k", 144), mb("B1", 144), 16384.0, A.mult)
     ts(mf("BO"), C("c4"), P(1), A.is_equal)
     ms(mf("ON"), 1.0)
-    ts(cf("M16", 96), C("kc", 0, 96), P(2), A.is_equal)
+    ts(cf("M16", 16), C("kc", 0, 16), P(2), A.is_equal)
     ts(cf("lf", 8), col(8), 16.0, A.mult, P(2), A.add)
     ts(cf("cT", 8), C("lf"), 2560.0, A.add)
     ts(cf("c15", 8), C("lf"), 16.0, A.mult, 15.0, A.add)
     ts(cf("hl", 8), C("lf"), 0.5, A.mult)
     ts(cf("c2", 8), C("lf"), -0.5, A.mult, 0.5, A.add)
-    ts(mb("FR", 144), mb("B1", 144), P(8), A.mult)
-    ts(mb("FR16", 144), mb("FR", 144), 16.0, A.mult)
+    ts(mb("I16"), mf("I"), 16.0, A.mult)
     ts(v("ks", 0, 128), C("kc"), P(2), A.is_equal)
     ts(v("ks", 128, 256), C("kc"), P(2), A.is_lt, -1.0, A.mult)
     for Q in range(2):
@@ -359,30 +359,25 @@ def rank_program(g, core, T, topo):
     ts(v("ks", 256, 768), col(512), P(16), A.is_equal)
     ts(v("ks", 768, 1280), col(512), P(17), A.is_equal)
     tt(mb("U", 512), v("ks", 256, 768), v("ks", 768, 1280), A.add)
-    ts(v("k4", 0, 96), col(96), 1600.0, A.add)
-    tt(cf("cxM", 96), v("k4", 0, 96), C("M16"), A.mult)
+    ms(v("P2", 96, 112), 4096.0)
     cp(v("jr"), col(192))
     ms(cf("one", 96), 1.0)
     ts(cf("jl", 12), col(12), 16.0, A.mult, P(2), A.add)
+    ts(cf("bj", 12), C("jl"), 0.5, A.add)
     ts(cf("jT", 12), C("jl"), 1536.0, A.add)
-    for i in range(8):
+    for i in range(12):
         ts(v("rr", 128 * i, 128 * i + 128), C("kc"), 0.0, A.is_gt, 64.0, A.mult)
-        ts(v("rr", 1024 + 128 * i, 1152 + 128 * i), C("kc"), 0.0, A.is_equal, 64.0, A.mult)
+        ts(v("rr", 1536 + 128 * i, 1664 + 128 * i), C("kc"), 0.0, A.is_equal, 64.0, A.mult)
 
     ADD, SUB, MUL, MAX, MIN = A.add, A.subtract, A.mult, A.max, A.min
     X, cot, sut = v("X", 0, 2560), v("cot"), v("sut")
     PART = {0: (0, NA), 1: (NA, 128)}
     PU = {1: "pF", 0: "pM"}
+    qv = lambda name, i, j=None: v(name, 512 * i, 512 * (i if j is None else j) + 512)
 
     def turn(src, nblk):
-        if MIX:
-            o, i = v3("t3", 32, 0, nblk), v(src, 0, 32 * nblk)
-            rec("V", [lambda: vec.transpose(o[0], i[0])], [i], [o], 32 * nblk * CY)
-            return
-        for a in range(nblk):
-            o = (T.t3[:, a, :], [("t3", 32 * a, 32 * a + 32, True)], 32)
-            i = v(src, 32 * a, 32 * a + 32)
-            rec("V", [lambda o=o, i=i: vec.transpose(o[0], i[0])], [i], [o], 64 * CY)
+        o, i = v3("t3", 32, 0, nblk), v(src, 0, 32 * nblk)
+        rec("V", [lambda: vec.transpose(o[0], i[0])], [i], [o], 32 * nblk * CY)
 
     def swap(nblk):
         for cpx in range(2):
@@ -390,35 +385,34 @@ def rank_program(g, core, T, topo):
                 [(mf("SW%d%d" % (cpx, gp)), v3("t3", 32, 0, nblk, 16 * gp, 16 * gp + 16)) for gp in range(2)], f32=True)
 
     def with_q(o, lo, hi, q0, b, op):
-        if MIX:
-            tt(v(o, lo, hi), v3("pQ", 32, (q0 + lo) // 32, (q0 + hi) // 32), b(lo, hi), op)
-            return
-        for c in range(lo // 16, hi // 16):
-            x = q0 // 16 + c
-            q = (T.pQ[:, x // 2, 16 * (x % 2):16 * (x % 2) + 16], [("pQ", 16 * x, 16 * x + 16, False)], 16)
-            tt(v(o, 16 * c, 16 * c + 16), q, b(16 * c, 16 * c + 16), op)
+        tt(v(o, lo, hi), v3("pQ", 32, (q0 + lo) // 32, (q0 + hi) // 32), b, op)
 
     def distance(pd, w, buf, part):
         c0 = 4 * part
         mms(v(pd, 0, NA), [(slide(w, m), v3(buf, 256, c0, c0 + 4, 16 * m, 16 * m + 16)) for m in range(16)])
 
-    BANK = ("pX2", "pM", "pX0", "pX1")
+    def shifted(o, z, lists, dx, part, zs):
+        qs = [i for i in (2 * part, 2 * part + 1) if i not in zs]
+        for i in (2 * part, 2 * part + 1):
+            if i in zs:
+                act(qv(z, i), ind(X, v(lists, 32 * i, 32 * i + 32)))
+                mms(v(BANK[i]), [(mb("I"), qv(z, i)), (mb("I"), qv(dx, i))])
+                ts(qv(o, i), v(BANK[i]), 0.0, MAX, 63.0, MIN)
+        if qs:
+            i, j = qs[0], qs[-1]
+            tt(qv(z, i, j), ind(X, v(lists, 32 * i, 32 * j + 32)), qv(dx, i, j), ADD)
+            ts(qv(o, i, j), qv(z, i, j), 0.0, MAX, 63.0, MIN)
 
-    def far(xb, eb, ab, lists, l0, quarters):
+    def apart(xb, db, eb, ab, lists, l0, quarters):
         for i in quarters:
-            act(v(xb, 512 * i, 512 * i + 512), ind(X, v(lists, l0 + 32 * i, l0 + 32 * i + 32)))
+            act(qv(xb, i), ind(X, v(lists, l0 + 32 * i, l0 + 32 * i + 32)))
         for i in quarters:
-            p = v(BANK[i])
-            mms(p, [(mb("I"), v(xb, 512 * i, 512 * i + 512)), (mb("nI"), v(eb, 512 * i, 512 * i + 512))])
-            act(v3(ab, 256, 2 * i, 2 * i + 2), p, F.Abs)
-
-    def near(eb, ab, db, lists, l0, quarters):
-        for i in quarters:
-            tt(v(db, 512 * i, 512 * i + 512), ind(X, v(lists, l0 + 32 * i, l0 + 32 * i + 32)), v(eb, 512 * i, 512 * i + 512), SUB)
-            act(v3(ab, 256, 2 * i, 2 * i + 2), v(db, 512 * i, 512 * i + 512), F.Abs)
-
-    def clip(o, z, part):
-        ts(v(o, EA * part, EA * part + EA), v(z, EA * part, EA * part + EA), 0.0, MAX, 63.0, MIN)
+            mms(v(BANK[i]), [(mb("I"), qv(xb, i)), (mb("nI"), qv(eb, i))])
+            act(v3(ab, 256, 2 * i, 2 * i + 2), v(BANK[i]), F.Abs)
+        for i in (3, 2, 0, 1):
+            if i not in quarters:
+                tt(qv(db, i), ind(X, v(lists, l0 + 32 * i, l0 + 32 * i + 32)), qv(eb, i), SUB)
+                act(v3(ab, 256, 2 * i, 2 * i + 2), qv(db, i), F.Abs)
 
     for t in range(RO):
         dx = "dx%d" % (t % 2)
@@ -426,29 +420,24 @@ def rank_program(g, core, T, topo):
         ab, here = v("abt", 16 * t, 16 * t + 16), [trip("ab%da" % t)]
         cp(v("dfk"), ind(cot, ab), here)
         for part in (1, 0):
-            lo, hi = PART[part]
-            tt(v("z", 16 * lo, 16 * hi), ind(X, v("dfk", lo, hi)), v(dx, 16 * lo, 16 * hi), ADD)
-            clip("e1", "z", part)
+            shifted("e1", "z", "dfk", dx, part, ZS1)
         cp(v("f2"), v("dfk"))
         turn("f2", 8)
-        far("xf", "e1", "a3", "dfk", 128, FAR1)
-        near("e1", "a3", "da", "dfk", 128, [i for i in (3, 2, 0, 1) if i not in FAR1])
+        apart("xf", "da", "e1", "a3", "dfk", 128, FAR1)
         swap(8)
         distance("pD1", "B1", "a3", 1)
         distance("pD0", "B1", "a3", 0)
-
         for part in (1, 0):
             lo, hi = PART[part]
             tt(v("key", lo, hi), v("pD%d" % part, 0, NA), C("k16", lo, hi), ADD)
             scan(v("sc", lo, hi), C("R1", lo, hi), v("key", lo, hi), MAX, MIN)
             for c in range(lo // 16, hi // 16):
                 ts(v("oh", 16 * c, 16 * c + 16), v("key", 16 * c, 16 * c + 16), v("sc", 16 * c + 15, 16 * c + 16), A.is_equal)
-            with_q("pr", lo, hi, 0, lambda a, b: v("oh", a, b), MUL)
+            with_q("pr", lo, hi, 0, v("oh", lo, hi), MUL)
             scan(v("ds", lo, hi), C("R3", lo, hi), v("pr", lo, hi), MUL, ADD)
             cp(v("d16", 4 * part, 4 * part + 4), v("ds", lo + 15, hi, 16))
             cp(v("sj", lo, hi), ind(sut, v("d16", 4 * part, 4 * part + 4)))
-            tt(v("z2", 16 * lo, 16 * hi), ind(X, v("sj", lo, hi)), v(dx, 16 * lo, 16 * hi), ADD)
-            clip("e", "z2", part)
+            shifted("e", "z2", "sj", dx, part, ZS2)
             mms(v(PU[part], 0, NA), [(slide("W", j), v("e", 16 * lo + j, 16 * hi, 16)) for j in range(16)])
             r = lambda k: v(k, lo, hi)
             cp(r("ui"), v(PU[part], 0, NA))
@@ -459,17 +448,16 @@ def rank_program(g, core, T, topo):
             ts(r("ni"), r("nn"), 5, A.arith_shift_right, 1023, A.bitwise_and)
             cp(r("n16"), r("ni"))
             cp(r("nf"), r("ni"))
-        with_q("prf", 0, 128, 128, lambda a, b: v("oh", a, b), MUL)
+        with_q("prf", 0, 128, 128, v("oh"), MUL)
         scan(v("fs"), C("R3"), v("prf"), MUL, ADD)
         ts(v("al"), v("sc", 15, 128, 16), v("thv"), A.is_lt)
         tt(v("alT"), v("al"), C("cT"), MUL)
-        far("xn", "e", "b3", "n16", 0, FAR2)
-        near("e", "b3", "db", "n16", 0, [i for i in (3, 2, 0, 1) if i not in FAR2])
+        apart("xn", "db", "e", "b3", "n16", 0, FAR2)
         turn("nf", 4)
         swap(4)
         distance("pD1", "B16k", "b3", 1)
         distance("pD0", "B16k", "b3", 0)
-        with_q("pay", 0, 128, 0, lambda a, b: C("pc2", a, b), ADD)
+        with_q("pay", 0, 128, 0, C("pc2"), ADD)
         for part in (1, 0):
             lo, hi = PART[part]
             tt(v("key2", lo, hi), v("pD%d" % part, 0, NA), v("pay", lo, hi), ADD)
@@ -498,7 +486,7 @@ def rank_program(g, core, T, topo):
         tt(v("q"), v("m128"), C("lf"), ADD)
         tt(v("nb"), C("c2"), v("m128"), SUB)
         for c in range(8):
-            act(v("nlx", 16 * c, 16 * c + 16), C("M16", 0, 16), F.Copy, scale=v("q", c, c + 1))
+            act(v("nlx", 16 * c, 16 * c + 16), C("M16"), F.Copy, scale=v("q", c, c + 1))
         mms(v("pM", 0, 128), [(mf("BO"), v("nlx"))], f32=True)
         for c in range(8):
             act(v("ab1", 128 * c, 128 * c + 16 * c + 16), v("pM", 0, 16 * c + 16), F.Abs, bias=v("nb", c, c + 1))
@@ -517,7 +505,11 @@ def rank_program(g, core, T, topo):
         ts(v("hi"), v("pX2", 0, 128), 1.0 / 32, MUL, 128.0 - 31.0 / 64, ADD)
         ts(v("hs"), v("hi"), -32.0, MUL, 4096.0, ADD)
         tt(v("lo"), v("pX2", 0, 128), v("hs"), ADD)
-        for h in range(48):
+        for h in range(48 - NS, 48):
+            act(v("sh", 128 * (h - 48 + NS), 128 * (h - 47 + NS)), v("hi"), F.Abs, bias=-160.0 - h)
+        for h in range(48 - NS, 48):
+            act(v("ohh", 128 * h, 128 * h + 128), v("sh", 128 * (h - 48 + NS), 128 * (h - 47 + NS)), F.Relu, bias=1.0, scale=-1.0)
+        for h in range(48 - NS):
             ts(v("ohh", 128 * h, 128 * h + 128), v("hi"), 160.0 + h, A.is_equal)
         for h in range(32):
             ts(v("ohl", 128 * h, 128 * h + 128), v("lo"), float(h), A.is_equal)
@@ -537,43 +529,33 @@ def rank_program(g, core, T, topo):
         for mi, bank in (("O", "pX0"), ("T", "pX1")) + ((("C", "pD0"),) if not last else ()):
             for b in range(2):
                 mms(v(bank, b, 96, 2), [(mb(mi + str(2 * Q + b)), v("Fl", 48 * Q, 48 * Q + 48)) for Q in range(2)])
-        tot = v("pX0", 0, 96)
-        scan(v("Sx"), C("one"), tot, MUL, ADD)
-        ts(v("em"), tot, 0.0, A.is_equal)
-        tt(v("tM"), tot, C("M16"), MUL)
-        tt(v("em"), v("em"), C("cxM"), MUL)
-        tt(v("em2"), v("em"), v("tM"), SUB)
-        tt(v("Ex"), v("Sx"), C("M16"), MUL)
-        tt(v("Ex"), v("Ex"), v("em2"), ADD)
-        scan(v("em"), C("R3", 0, 96), v("Ex"), MUL, ADD)
-        cp(v("sl16", 0, 6), v("em", 15, 96, 16))
-        tt(v("P2"), v("Sx"), v("pX1", 0, 96), ADD)
-        ms(v("Am", 0, 192), 0.0)
-        scatter(v("Am"), v("sl16", 0, 6), v("jr", 0, 96))
-        scan(v("xr"), v("Am", 0, 192), v("Am", 0, 192), MAX, MAX)
-        mms(v("pX2", 0, 12), [(slide("FR", m), v("xr", m, 192, 16)) for m in range(16)])
-        cp(v("xl"), v("pX2", 0, 12))
-        mms(v("pD1", 0, 12), [(slide("FR16", m), v("xr", m, 192, 16)) for m in range(16)], True, False)
+        scan(v("Sx"), C("one"), v("pX0", 0, 96), MUL, ADD)
+        for c in range(12):
+            act(v("sg", 96 * c, 96 * c + 96), v("Sx"), F.Sign, bias=C("bj", c, c + 1), scale=-1.0, acc=v("xa", c, c + 1))
+        tt(v("P2", 0, 96), v("Sx"), v("pX1", 0, 96), ADD)
+        ts(v("xl"), v("xa"), 0.5, MUL, 48.0, ADD)
+        ts(v("xb"), v("xa"), 0.5, MUL, 48.0, ADD)
         tt(v("cm"), ind(v("P2"), v("xl")), v("jr"), A.is_le)
-        mms(v("pD1", 0, 12), [(slide("B1", m), v("cm", m, 192, 16)) for m in range(16)], False, True)
+        mms(v("pD1", 0, 12), [(mb("I16"), v("xb"))] + [(slide("B1", m), v("cm", m, 192, 16)) for m in range(16)])
         ts(v("no16"), v("pD1", 0, 12), 1024.0, ADD)
         cp(v("s4"), ind(sut, v("no16")))
-        for c in (1, 2):
-            act(v("R", 1024 * c, 1024 * c + 1024), ind(X, v("s4", 64 * c, 64 * c + 64)))
-        cp(v("R", 0, 1024), ind(X, v("s4", 0, 64)))
+        cut = [sum(RC[:i]) for i in range(len(RC) + 1)]
+        for lo, hi in zip(cut[1:], cut[2:]):
+            act(v("R", 16 * lo, 16 * hi), ind(X, v("s4", lo, hi)))
+        cp(v("R", 0, 16 * cut[1]), ind(X, v("s4", 0, cut[1])))
         ts(v("iv"), C("jl"), v("Sx", 95, 96), A.is_ge)
         tt(v("iv"), v("iv"), C("jT"), MUL)
         tt(v("vl"), v("pD1", 0, 12), v("iv"), MAX)
         cp(v("vl16"), v("vl"))
         if not last:
-            ts(v("g2"), v("P2"), 192.0, A.is_gt)
+            ts(v("g2"), v("P2", 0, 96), 192.0, A.is_gt)
             tt(v("old"), v("pD0", 0, 96), v("g2"), MUL)
-        for c in range(3):
-            r = v("R", 1024 * c, 1024 * c + 1024)
-            scan(v("mx", 1024 * c, 1024 * c + 1024), v("rr", 0, 1024), r, MIN, MAX)
-            scan(v("mn", 1024 * c, 1024 * c + 1024), v("rr", 1024, 2048), r, MAX, MIN)
-            tt(v("sm", 64 * c, 64 * c + 64), v("mx", 1024 * c + 15, 1024 * c + 1024, 16), v("mn", 1024 * c + 15, 1024 * c + 1024, 16), ADD)
-            ts(v("vi", 64 * c, 64 * c + 64), v("sm", 64 * c, 64 * c + 64), 0.5, MUL, -0.25, ADD)
+        for lo, hi in zip(cut, cut[1:]):
+            n, r = 16 * (hi - lo), v("R", 16 * lo, 16 * hi)
+            scan(v("mx", 16 * lo, 16 * hi), v("rr", 0, n), r, MIN, MAX)
+            scan(v("mn", 16 * lo, 16 * hi), v("rr", 1536, 1536 + n), r, MAX, MIN)
+            tt(v("sm", lo, hi), v("mx", 16 * lo + 15, 16 * hi, 16), v("mn", 16 * lo + 15, 16 * hi, 16), ADD)
+            ts(v("vi", lo, hi), v("sm", lo, hi), 0.5, MUL, -0.25, ADD)
         scatter(v("X", 1024, XW), v("vl16"), v("vi"))
     store("stx1", T.yx[:, 1024:2560], v("X", 1024, 2560))
     flush()

@@ -4,9 +4,10 @@ XW = 2752
 CW = 2688
 NA = 64
 RO = 4
-ZS1, ZS2 = (1,), (1,)
-FAR1, FAR2 = (2, 3), (2,)
-NS = 14
+ZS1, ZS2 = (1, 3), (1, 3)
+FAR1, FAR2 = (2, 3), (2, 3)
+NS = 12
+NV = 4
 RC = (48, 80, 64)
 
 _B, _F, _I, _U = "bfloat16", "float32", "int32", "uint16"
@@ -22,14 +23,14 @@ _S = {
     "m128": (8, _F), "q": (8, _F), "nb": (8, _F), "cg": (128, _F), "nlx": (128, _F), "esel": (128, _B),
     "hi": (128, _B), "hs": (128, _B), "lo": (128, _B), "sh": (2048, _B), "ohl": (4096, _B), "ohh": (6144, _B),
     "ab1": (1024, _F), "rl": (1024, _F), "los": (8, _F), "lt": (8, _F), "tg": (8, _F), "tg16": (8, _U),
-    "Fl": (96, _B), "Sx": (96, _F), "P2": (112, _B), "sg": (1152, _B), "xa": (12, _F), "xb": (12, _B), "xl": (12, _U),
+    "Fq": (256, _B), "Fl": (96, _B), "Sx": (96, _F), "P2": (112, _B), "sg": (1152, _B), "xa": (12, _F), "xb": (12, _B), "xl": (12, _U),
     "cm": (192, _B), "no16": (12, _U), "s4": (192, _U),
     "R": (3072, _B), "mx": (3072, _B), "mn": (3072, _B), "sm": (192, _F), "vi": (192, _I),
     "iv": (12, _F), "vl": (12, _F), "vl16": (12, _U), "g2": (96, _B), "old": (96, _B),
     "al": (8, _F), "alT": (8, _F), "af": (16, _F), "u8": (16, _F), "abf": (16, _F),
     "cnt": (1, _F), "ai": (1, _I), "thb": (1, _F), "thv": (1, _F), "th8": (1, _F),
-    "pc": (24, _F), "ci": (160, _I), "cf": (1408, _F), "mf": (1024, _F), "mb": (3024, _B), "rr": (3072, _B), "tmp": (512, _F), "jr": (192, _B),
-    "ks": (1280, _F), "k4": (128, _F),
+    "pc": (24, _F), "ci": (160, _I), "cf": (1408, _F), "mf": (1024, _F), "mb": (3024, _B), "rr": (3072, _B), "tmp": (256, _F), "jr": (192, _B),
+    "ks": (128, _F), "k4": (128, _F),
 }
 SCRATCH = {k: ("sbuf", [128, n], d) for k, (n, d) in _S.items()}
 SCRATCH["a3"] = ("sbuf", [128, 8, 256], _B)
@@ -43,7 +44,7 @@ BANK = ("pX2", "pM", "pX0", "pX1")
 LOADS = ["ldla", "ldlb", "ldco", "ldsu", "lddl", "ldx", "ldwt", "ldth"]
 STORES = ["stx0", "stx1", "sta", "stb"]
 SEMAPHORES = ["sV", "sS", "sP", "sG", "loc", "ab1a", "ab2a", "ab3a", "dl1a", "dl2a", "dl3a"] + LOADS + STORES
-CY, PCY, GAT, SCT, WAKE = 0.00104, 0.0007, 1.5, 3.5, 0.08
+CY, PCY, GAT, SCT, WAKE = 0.00104, 0.0005, 1.5, 3.5, 0.12
 
 
 def rank_program(g, core, T, topo):
@@ -210,6 +211,9 @@ def rank_program(g, core, T, topo):
     def ms(o, c):
         rec("V", [lambda: vec.memset(o[0], c)], [], [o], max(64, o[2]) * CY)
 
+    def total(o, a):
+        rec("V", [lambda: vec.tensor_reduce(o[0], a[0], AxisListType.X, A.add)], [a], [o], max(64, a[2]) * CY)
+
     def scan(o, a, b, op0, op1):
         rec("V", [lambda: vec.tensor_tensor_scan(o[0], a[0], b[0], 0.0, op0, op1)], [a, b], [o], vcost(o, b, 0.5 if small(o, a, b) else 1))
 
@@ -278,9 +282,20 @@ def rank_program(g, core, T, topo):
 
     spread(0)
 
-    iota(v("ci", 0, 128), [[1, 128]], 0, 0)
+    CF, at = {}, [0]
+
+    def cf(k, n):
+        CF[k] = (at[0], n)
+        at[0] += n
+        return v("cf", CF[k][0], CF[k][0] + n)
+
+    C = lambda k, lo=0, hi=None: v("cf", CF[k][0] + lo, CF[k][0] + (CF[k][1] if hi is None else hi))
+    SM = {"allow_small_or_imprecise_dtypes": True}
+    iota(v("tmp"), [[1, 256]], 0, 0, **SM)
     iota(v("ci", 128, 129), [[0, 1]], 0, 1)
-    iota(v("tmp"), [[1, 512]], 0, 0, allow_small_or_imprecise_dtypes=True)
+    iota(cf("kc", 128), [[0, 8], [1, 16]], 0, 0, **SM)
+    iota(cf("c4", 128), [[1, 8], [0, 16]], 0, 0, **SM)
+    iota(v("jr"), [[1, 192]], 0, 0, **SM)
     col = lambda n: v("tmp", 0, n)
     cp(v("abt", 0, 16), lab)
     ms(v("cot", 2560, CW), 0)
@@ -296,26 +311,16 @@ def rank_program(g, core, T, topo):
     ts(P(6), P(3), 4.0, A.add)
     tt(P(9), P(0), P(2), A.subtract)
     ts(P(10), P(9), 15.0, A.add)
-    MB = {"B1": 0, "B16k": 144, "W": 288, "I16": 432, "I": 720, "nI": 848, "U": 976}
+    MB = {"B1": 0, "B16k": 144, "W": 288, "I16": 432, "E": 560, "I": 720, "nI": 848, "U": 976}
     for i, k in enumerate(("T", "O", "C")):
         for b in range(4):
             MB[k + str(b)] = 1488 + 128 * (4 * i + b)
     mb = lambda k, n=128: v("mb", MB[k], MB[k] + n)
     slide = lambda k, m: v("mb", MB[k] + 15 - m, MB[k] + 143 - m)
-    CF, at = {}, [0]
-
-    def cf(k, n):
-        CF[k] = (at[0], n)
-        at[0] += n
-        return v("cf", CF[k][0], CF[k][0] + n)
-
-    C = lambda k, lo=0, hi=None: v("cf", CF[k][0] + lo, CF[k][0] + (CF[k][1] if hi is None else hi))
     MF = {"I": 0, "BO": 128, "ON": 256, "E8": 384, "SW00": 512, "SW01": 640, "SW10": 768, "SW11": 896}
     mf = lambda k: v("mf", MF[k], MF[k] + 128)
     ts(mb("B1", 144), col(144), P(10), A.is_equal)
-    ts(v("ci", 0, 128), v("ci", 0, 128), 15, A.bitwise_and)
-    cp(cf("kc", 128), v("ci", 0, 128))
-    ts(cf("k16", 128), C("kc"), 1.0 / 16, A.mult)
+    act(cf("k16", 128), C("kc"), scale=1.0 / 16)
     ts(cf("R1", 128), C("kc"), 0.0, A.is_equal, 32768.0, A.mult)
     ts(cf("R3", 128), C("kc"), 0.0, A.is_gt)
     ts(mf("I"), col(128), P(0), A.is_equal)
@@ -323,11 +328,9 @@ def rank_program(g, core, T, topo):
         for gp in range(2):
             ts(P(11 + 2 * cpx + gp), P(0), 16.0 * (gp - cpx), A.add)
             ts(mf("SW%d%d" % (cpx, gp)), col(128), P(11 + 2 * cpx + gp), A.is_equal, P(4 + cpx), A.mult)
-    cp(mb("I"), mf("I"))
-    ts(mb("nI"), mf("I"), -1.0, A.mult)
+    act(mb("I"), mf("I"))
+    act(mb("nI"), mf("I"), scale=-1.0)
     ts(mb("W", 144), mb("B1", 144), v("wtc"), A.mult)
-    tt(v("k4"), col(128), C("kc"), A.subtract)
-    ts(cf("c4", 128), v("k4"), 1.0 / 16, A.mult)
     ts(mf("E8"), C("c4"), P(0), A.is_equal)
     th8 = v("th8", 0, 1, 1, (0, 8))
     cp(th8, v("thi", 0, 1, 1, (0, 8)))
@@ -335,8 +338,8 @@ def rank_program(g, core, T, topo):
     cp(v("thb"), v("pM", 0, 1))
     cp(v("thv"), v("thb"))
     ts(cf("R2", 128), C("kc"), 0.0, A.is_gt, 16777216.0, A.mult)
-    ts(cf("pc2", 128), C("kc"), -1024.0, A.mult, 15360.0, A.add)
-    ts(mb("B16k", 144), mb("B1", 144), 16384.0, A.mult)
+    act(cf("pc2", 128), C("kc"), F.Identity, bias=15360.0, scale=-1024.0)
+    act(mb("B16k", 144), mb("B1", 144), scale=16384.0)
     ts(mf("BO"), C("c4"), P(1), A.is_equal)
     ms(mf("ON"), 1.0)
     ts(cf("M16", 16), C("kc", 0, 16), P(2), A.is_equal)
@@ -345,29 +348,32 @@ def rank_program(g, core, T, topo):
     ts(cf("c15", 8), C("lf"), 16.0, A.mult, 15.0, A.add)
     ts(cf("hl", 8), C("lf"), 0.5, A.mult)
     ts(cf("c2", 8), C("lf"), -0.5, A.mult, 0.5, A.add)
-    ts(mb("I16"), mf("I"), 16.0, A.mult)
-    ts(v("ks", 0, 128), C("kc"), P(2), A.is_equal)
-    ts(v("ks", 128, 256), C("kc"), P(2), A.is_lt, -1.0, A.mult)
+    act(mb("I16"), mf("I"), scale=16.0)
+    ts(v("ks"), C("kc"), P(2), A.is_lt, -1.0, A.mult)
+    ts(P(18), P(3), 16.0, A.mult, P(2), A.add)
+    ts(P(19), P(18), 64.0, A.add)
     for Q in range(2):
         for b in range(2):
             i = str(2 * Q + b)
             ts(mb("O" + i), C("c4"), P(6 if Q else 3), A.is_equal, P(4 + b), A.mult)
-            tt(mb("C" + i), mb("O" + i), v("ks", 0, 128), A.mult)
-            tt(mb("T" + i), mb("O" + i), v("ks", 128, 256), A.mult)
-    ts(P(16), P(1), 64.0, A.mult, P(2), A.add)
-    ts(P(17), P(16), 48.0, A.add)
-    ts(v("ks", 256, 768), col(512), P(16), A.is_equal)
-    ts(v("ks", 768, 1280), col(512), P(17), A.is_equal)
-    tt(mb("U", 512), v("ks", 256, 768), v("ks", 768, 1280), A.add)
+            ts(mb("C" + i), col(128), P(18 + Q), A.is_equal, P(4 + b), A.mult)
+            tt(mb("T" + i), mb("O" + i), v("ks"), A.mult)
+    ts(P(16), P(1), 32.0, A.mult, P(2), A.add)
+    ts(P(17), P(16), 16.0, A.add)
+    for b in range(2):
+        ts(v("mb", MB["U"] + 256 * b, MB["U"] + 256 * b + 256), col(256), P(16 + b), A.is_equal)
+    for Q in range(2):
+        ts(v("k4", 48 * Q, 48 * Q + 48), col(48), 2.0, A.mult, float(Q), A.add)
+        ts(v("mb", MB["E"] + 48 * Q, MB["E"] + 48 * Q + 48), v("k4", 48 * Q, 48 * Q + 48), P(0), A.is_equal)
     ms(v("P2", 96, 112), 4096.0)
-    cp(v("jr"), col(192))
     ms(cf("one", 96), 1.0)
     ts(cf("jl", 12), col(12), 16.0, A.mult, P(2), A.add)
     ts(cf("bj", 12), C("jl"), 0.5, A.add)
     ts(cf("jT", 12), C("jl"), 1536.0, A.add)
-    for i in range(12):
-        ts(v("rr", 128 * i, 128 * i + 128), C("kc"), 0.0, A.is_gt, 64.0, A.mult)
-        ts(v("rr", 1536 + 128 * i, 1664 + 128 * i), C("kc"), 0.0, A.is_equal, 64.0, A.mult)
+    for x, op in ((0, A.is_gt), (1536, A.is_equal)):
+        ts(v("rr", x, x + 128), C("kc"), 0.0, op, 64.0, A.mult)
+        for n, m in ((128, 128), (256, 256), (512, 512), (1024, 512)):
+            act(v("rr", x + n, x + n + m), v("rr", x, x + m))
 
     ADD, SUB, MUL, MAX, MIN = A.add, A.subtract, A.mult, A.max, A.min
     X, cot, sut = v("X", 0, 2560), v("cot"), v("sut")
@@ -471,7 +477,7 @@ def rank_program(g, core, T, topo):
         if not last:
             cp(v("abo", 16 * t, 16 * t + 16), v("abf"))
             remote(T.cores[(rank + 1) % N], "abt", 16 * t + 16, 16 * t + 32, v("abo", 16 * t, 16 * t + 16), "ab%da" % (t + 1))
-            rec("V", [lambda: vec.tensor_reduce(T.cnt[:, 0:1], T.al[:, 0:8], AxisListType.X, ADD)], [v("al")], [v("cnt")], 64 * CY)
+            total(v("cnt"), v("al"))
         else:
             store("sta", T.ya[:], v("abf", 0, 8))
             store("stb", T.yb[:], v("abf", 8, 16))
@@ -513,28 +519,36 @@ def rank_program(g, core, T, topo):
             ts(v("ohh", 128 * h, 128 * h + 128), v("hi"), 160.0 + h, A.is_equal)
         for h in range(32):
             ts(v("ohl", 128 * h, 128 * h + 128), v("lo"), float(h), A.is_equal)
-        for gi in range(8):
+        for pr in range(4):
+            o, fq = v(("pF", "pX0", "pX1", "pD0")[pr], 0, 64, 1, (0, 96)), v("Fq", 64 * pr, 64 * pr + 64, 1, (0, 96))
+            mms(o, [(v("ohh", 16 * pr + k, 6144, 64), v("ohl", 16 * pr + k, 4096, 64)) for k in range(16)])
+            ts(fq, o, 0.0, A.is_gt)
+        for gi in (0, 4, 1, 5, 2, 6, 3, 7):
             Q, q4 = divmod(gi, 4)
-            pairs = [(v("ohl", 16 * gi + k, 4096, 128), v("ohh", 16 * gi + k, 6144, 128)) for k in range(16)]
+            pairs = [(v("Fq", 64 * q4 + Q, 64 * q4 + 64, 2, (0, 96)), v("mb", MB["E"] + 48 * Q, MB["E"] + 48 * Q + 48, 1, (0, 96)))]
             if t:
-                pairs += [(v("mb", MB["U"] + 64 * gi + 32 * b, MB["U"] + 64 * gi + 32 * b + 32), v("old", b, 96, 2)) for b in range(2)]
-            mms(v("pF", 48 * Q, 48 * Q + 48, 1, (32 * q4, 32 * q4 + 32)), pairs)
+                pairs = [(v("mb", MB["U"] + 256 * b + 32 * gi, MB["U"] + 256 * b + 32 * gi + 32), v("old", b, 96, 2)) for b in range(2)] + pairs
+            mms(v("pD1", 48 * Q, 48 * Q + 48, 1, (32 * q4, 32 * q4 + 32)), pairs)
         if not last:
             spread(t + 1)
             mms(v("pM", 0, 1), [(mf("ON"), v("cnt"))], f32=True)
             ts(v("ai"), v("pM", 0, 1), -1.0, MUL, 1024.0, ADD)
             ts(v("ai"), v("ai"), 63, A.bitwise_and)
             tt(v("thv"), v("thb"), v("ai"), ADD)
-        ts(v("Fl"), v("pF", 0, 96), 0.0, A.is_gt)
+        ts(v("Fl"), v("pD1", 0, 96), 0.0, A.is_gt)
         for mi, bank in (("O", "pX0"), ("T", "pX1")) + ((("C", "pD0"),) if not last else ()):
             for b in range(2):
                 mms(v(bank, b, 96, 2), [(mb(mi + str(2 * Q + b)), v("Fl", 48 * Q, 48 * Q + 48)) for Q in range(2)])
         scan(v("Sx"), C("one"), v("pX0", 0, 96), MUL, ADD)
-        for c in range(12):
+        for c in range(12 - NV, 12):
+            ts(v("sg", 96 * c, 96 * c + 96), v("Sx"), C("bj", c, c + 1), A.is_lt)
+            total(v("xa", c, c + 1), v("sg", 96 * c, 96 * c + 96))
+        for c in range(12 - NV):
             act(v("sg", 96 * c, 96 * c + 96), v("Sx"), F.Sign, bias=C("bj", c, c + 1), scale=-1.0, acc=v("xa", c, c + 1))
         tt(v("P2", 0, 96), v("Sx"), v("pX1", 0, 96), ADD)
-        ts(v("xl"), v("xa"), 0.5, MUL, 48.0, ADD)
-        ts(v("xb"), v("xa"), 0.5, MUL, 48.0, ADD)
+        for x in ("xl", "xb"):
+            ts(v(x, 0, 12 - NV), v("xa", 0, 12 - NV), 0.5, MUL, 48.0, ADD)
+            cp(v(x, 12 - NV, 12), v("xa", 12 - NV, 12))
         tt(v("cm"), ind(v("P2"), v("xl")), v("jr"), A.is_le)
         mms(v("pD1", 0, 12), [(mb("I16"), v("xb"))] + [(slide("B1", m), v("cm", m, 192, 16)) for m in range(16)])
         ts(v("no16"), v("pD1", 0, 12), 1024.0, ADD)

from concourse.mybir import dt, AluOpType as A, AxisListType, ActivationFunctionType as F

XW = 2752
CW = 2688
NA = 64
RO = 4
ZS1, ZS2 = (1, 3), (1, 3)
FAR1, FAR2 = (2, 3), (2, 3)
NS = 12
NV = 4
RC = (48, 80, 64)

_B, _F, _I, _U = "bfloat16", "float32", "int32", "uint16"
_S = {
    "X": (XW, _B), "cot": (CW, _I), "sut": (CW, _I), "dls": (512, _B), "dx0": (2048, _B), "dx1": (2048, _B),
    "abt": (64, _U), "abo": (64, _U), "lab": (16, _I), "wtc": (1, _B), "thi": (1, _I),
    "dfk": (256, _U), "f2": (256, _F), "xf": (2048, _B), "xn": (2048, _B), "z": (2048, _B), "z2": (2048, _B), "e1": (2048, _B), "e": (2048, _B),
    "da": (2048, _B), "db": (2048, _B),
    "key": (128, _F), "sc": (128, _F), "oh": (128, _F), "pr": (128, _F), "ds": (128, _F), "prf": (128, _F), "fs": (128, _F),
    "key2": (128, _F), "sc2": (128, _F), "d16": (16, _U), "sj": (128, _U), "ui": (128, _I), "uv": (128, _I), "w1": (128, _F), "w2": (128, _F), "nn": (128, _I),
    "ni": (128, _I), "n16": (128, _U), "nf": (128, _F), "pay": (128, _F),
    "k8": (8, _I), "n8": (8, _I), "j8": (8, _I), "nm": (8, _F), "nl": (8, _U), "jf": (8, _F), "jl": (8, _U),
    "m128": (8, _F), "q": (8, _F), "nb": (8, _F), "cg": (128, _F), "nlx": (128, _F), "esel": (128, _B),
    "hi": (128, _B), "hs": (128, _B), "lo": (128, _B), "sh": (2048, _B), "ohl": (4096, _B), "ohh": (6144, _B),
    "ab1": (1024, _F), "rl": (1024, _F), "los": (8, _F), "lt": (8, _F), "tg": (8, _F), "tg16": (8, _U),
    "Fq": (256, _B), "Fl": (96, _B), "Sx": (96, _F), "P2": (112, _B), "sg": (1152, _B), "xa": (12, _F), "xb": (12, _B), "xl": (12, _U),
    "cm": (192, _B), "no16": (12, _U), "s4": (192, _U),
    "R": (3072, _B), "mx": (3072, _B), "mn": (3072, _B), "sm": (192, _F), "vi": (192, _I),
    "iv": (12, _F), "vl": (12, _F), "vl16": (12, _U), "g2": (96, _B), "old": (96, _B),
    "al": (8, _F), "alT": (8, _F), "af": (16, _F), "u8": (16, _F), "abf": (16, _F),
    "cnt": (1, _F), "ai": (1, _I), "thb": (1, _F), "thv": (1, _F), "th8": (1, _F),
    "pc": (24, _F), "ci": (160, _I), "cf": (1408, _F), "mf": (1024, _F), "mb": (3024, _B), "rr": (3072, _B), "tmp": (256, _F), "jr": (192, _B),
    "ks": (128, _F), "k4": (128, _F),
}
SCRATCH = {k: ("sbuf", [128, n], d) for k, (n, d) in _S.items()}
SCRATCH["a3"] = ("sbuf", [128, 8, 256], _B)
SCRATCH["b3"] = ("sbuf", [128, 8, 256], _B)
SCRATCH["t3"] = ("sbuf", [128, 8, 32], _F)
PSUM = ("pX0", "pX1", "pX2", "pD0", "pD1", "pF", "pM", "pQ")
for _k in PSUM[:7]:
    SCRATCH[_k] = ("psum", [128, 512], _F)
SCRATCH["pQ"] = ("psum", [128, 16, 32], _F)
BANK = ("pX2", "pM", "pX0", "pX1")
LOADS = ["ldla", "ldlb", "ldco", "ldsu", "lddl", "ldx", "ldwt", "ldth"]
STORES = ["stx0", "stx1", "sta", "stb"]
SEMAPHORES = ["sV", "sS", "sP", "sG", "loc", "ab1a", "ab2a", "ab3a", "dl1a", "dl2a", "dl3a"] + LOADS + STORES
CY, PCY, GAT, SCT, WAKE = 0.00104, 0.0005, 1.5, 3.5, 0.12


def rank_program(g, core, T, topo):
    rank = T.rank_of(core)
    if rank is None:
        return
    N = len(T.cores)
    que = {"V": g.vector, "S": g.scalar, "P": g.tensor, "G": g, "Y": g.sync}
    cnt = {"V": 0, "S": 0, "P": 0, "G": 0}
    known = {k: {} for k in que}
    snap, hist, ops = {}, {}, []

    def v(name, lo=0, hi=None, step=1, p=None):
        hi = (_S[name][0] if name in _S else 512) if hi is None else hi
        ps = slice(0, 128) if p is None else slice(p[0], p[1])
        ap = T[name][ps, lo:hi] if step == 1 else T[name][ps, lo:hi:step]
        return (ap, [(name, lo, hi, step == 1 and p is None)], -(-(hi - lo) // step))

    def v3(name, w, c0, c1, k0=0, k1=None):
        k1 = w if k1 is None else k1
        return (T[name][:, c0:c1, k0:k1], [(name, w * c0, w * c1, k0 == 0 and k1 == w)], (c1 - c0) * (k1 - k0))

    def ind(win, off):
        return (win[0].indirect(off[0]), win[1] + off[1], 16 * off[2])

    def clash(eng, b, lo, hi, isw, e2, w2, l2, h2):
        if b in PSUM and e2 != eng:
            return 2
        if b in PSUM and e2 == "P":
            return 1
        return 2 if (isw or w2) and lo < h2 and l2 < hi else 0

    def need_of(eng, acc):
        need = {}
        for (b, lo, hi, _c, isw) in acc:
            for (e2, c2, w2, l2, h2) in hist.get(b, ()):
                if need.get(e2, 0) < c2 and clash(eng, b, lo, hi, isw, e2, w2, l2, h2) == 2:
                    need[e2] = c2
        return need

    def sem_of(e):
        return T.sem["s" + e] if e in ("V", "S", "P", "G") else T.sem[e]

    def wait(eng, need):
        for e2 in sorted(need, key=lambda e: (e != eng, e)):
            c2 = need[e2]
            if known[eng].get(e2, 0) < c2:
                que[eng].wait_ge(sem_of(e2), c2)
                for k, n in snap.get((e2, c2), {}).items():
                    if known[eng].get(k, 0) < n:
                        known[eng][k] = n
                known[eng][e2] = c2

    def note(e, c, acc):
        for (b, lo, hi, full, isw) in acc:
            h = hist.setdefault(b, [])
            h[:] = [x for x in h if not (((isw and full) or (x[0] == e and x[2] == isw)) and lo <= x[3] and x[4] <= hi)]
            h.append((e, c, isw, lo, hi))

    def accs(rd, wr):
        return [a + (False,) for x in rd for a in x[1]] + [a + (True,) for x in wr for a in x[1]]

    def rec(eng, fns, rd, wr, cost, sem=None):
        ops.append((eng, fns, accs(rd, wr), cost, sem))

    def issue(op):
        eng, fns, acc, cost, sem = op
        wait(eng, need_of(eng, acc))
        if sem is None:
            for fn in fns:
                cnt[eng] += 1
                fn().then_inc(sem_of(eng), 1)
            s = dict(known[eng])
            s[eng] = cnt[eng] - 1
            snap[(eng, cnt[eng])] = s
            note(eng, cnt[eng], acc)
        elif sem == "remote":
            fns[0]()
        else:
            fns[0]().then_inc(T.sem[sem], 16)
            snap[(sem, 16)] = dict(known[eng])
            note(sem, 16, acc)

    def flush():
        n = len(ops)
        succ, npred, h2 = [[] for _ in range(n)], [0] * n, {}
        for i, (eng, _f, acc, cost, _s) in enumerate(ops):
            pred = {}
            for (b, lo, hi, _c, isw) in acc:
                for (j, e2, w2, l2, hh) in h2.get(b, ()):
                    c = clash(eng, b, lo, hi, isw, e2, w2, l2, hh)
                    if c and pred.get(j, 0) < c:
                        pred[j] = c
            for (b, lo, hi, full, isw) in acc:
                h = h2.setdefault(b, [])
                if isw and full and b not in PSUM:
                    h[:] = [x for x in h if not (lo <= x[3] and x[4] <= hi)]
                elif b in PSUM and len(h) > 60:
                    del h[:-60]
                h.append((i, eng, isw, lo, hi))
            for j, c in pred.items():
                if j != i:
                    succ[j].append((i, WAKE if c == 2 else 0.0))
                    npred[i] += 1
        prio = [0.0] * n
        for i in range(n - 1, -1, -1):
            prio[i] = ops[i][3] + max([prio[j] + w for j, w in succ[i]] + [0.0])
        ready, free = [0.0] * n, {k: 0.0 for k in que}
        avail = {k: [] for k in que}
        for i in range(n):
            if not npred[i]:
                avail[ops[i][0]].append(i)
        done = 0
        while done < n:
            best = None
            for e in que:
                if avail[e]:
                    t0 = max(free[e], min(ready[i] for i in avail[e]))
                    i = max((i for i in avail[e] if ready[i] <= t0), key=lambda i: (prio[i], -i))
                    if best is None or t0 < best[0]:
                        best = (t0, e, i)
            t0, e, i = best
            avail[e].remove(i)
            free[e] = t0 + (ops[i][3] if ops[i][4] is None else 0.1)
            for j, w in succ[i]:
                ready[j] = max(ready[j], t0 + ops[i][3] + w)
                npred[j] -= 1
                if not npred[j]:
                    avail[ops[j][0]].append(j)
            issue(ops[i])
            done += 1
        del ops[:]

    isv = lambda x: isinstance(x, tuple)
    raw = lambda x: x[0] if isv(x) else x
    vec, sca, ten = g.vector, g.scalar, g.tensor
    small = lambda *xs: all(SCRATCH[x[1][0][0]][2] in (_B, _U) for x in xs)
    isind = lambda x: len(x[1]) > 1
    inps = lambda x: x[1][0][0] in PSUM

    def vcost(o, a, k=1.0):
        if isind(a):
            return 0.05 + GAT * CY * o[2]
        return max(64, k * o[2]) * CY

    def tt(o, a, b, op):
        k = 1 if inps(a) or inps(b) else 2
        rec("V", [lambda: vec.tensor_tensor(o[0], a[0], b[0], op)], [a, b], [o], vcost(o, a, k))

    def ts(o, a, s1, op0, s2=None, op1=None):
        rd = [a] + [x for x in (s1, s2) if isv(x)]
        c = vcost(o, a, 0.5 if small(o, a) else 1)
        if op1 is None:
            rec("V", [lambda: vec.tensor_scalar(o[0], a[0], raw(s1), None, op0)], rd, [o], c)
        else:
            rec("V", [lambda: vec.tensor_scalar(o[0], a[0], raw(s1), raw(s2), op0, op1)], rd, [o], c)

    def cp(o, a, after=()):
        rec("V", [lambda: vec.tensor_copy(o[0], a[0])], [a] + list(after), [o], vcost(o, a, 0.5 if small(o, a) else 1))

    def scatter(win, off, a):
        rec("V", [lambda: vec.tensor_copy(win[0].indirect(off[0]), a[0])], [a, off], [win], 0.05 + SCT * CY * a[2])

    def ms(o, c):
        rec("V", [lambda: vec.memset(o[0], c)], [], [o], max(64, o[2]) * CY)

    def total(o, a):
        rec("V", [lambda: vec.tensor_reduce(o[0], a[0], AxisListType.X, A.add)], [a], [o], max(64, a[2]) * CY)

    def scan(o, a, b, op0, op1):
        rec("V", [lambda: vec.tensor_tensor_scan(o[0], a[0], b[0], 0.0, op0, op1)], [a, b], [o], vcost(o, b, 0.5 if small(o, a, b) else 1))

    def act(o, a, f=F.Copy, bias=None, scale=None, acc=None):
        rd = [a] + [x for x in (bias, scale) if isv(x)]
        kw = {}
        if bias is not None:
            kw["bias"] = raw(bias)
        if scale is not None:
            kw["scale"] = raw(scale)
        if acc is not None:
            kw["accum_out"] = acc[0]
        rec("S", [lambda: sca.activation(o[0], a[0], f, **kw)], rd, [o] + ([acc] if acc is not None else []), vcost(o, a))

    def mms(o, pairs, start=True, stop=True, f32=False):
        n = len(pairs)
        fns = [(lambda l=l, r=r, i=i: ten.matmul(o[0], l[0], r[0], start and i == 0, stop and i == n - 1)) for i, (l, r) in enumerate(pairs)]
        rd = {}
        for l, r in pairs:
            for x in (l, r):
                for (b, lo, hi, c) in x[1]:
                    q = rd.get(b, (lo, hi))
                    rd[b] = (min(lo, q[0]), max(hi, q[1]))
        cost = sum(max(min(64, l[2]), r[2]) for l, r in pairs) * PCY * (4 if f32 else 1)
        rec("P", fns, [(None, [(b, lo, hi, False)], 0) for b, (lo, hi) in rd.items()], [o], cost)

    def iota(o, pat, base, cm, **kw):
        rec("G", [lambda: g.iota(o[0], pat, base, cm, **kw)], [], [o], 0.13 + 2 * CY * o[2])

    def load(eng, name, o, src, after=()):
        rec(eng, [lambda: que[eng].dma_start(o[0], src[:])], list(after), [o], 3.0 + o[2] * 0.0015, name)

    def store(name, dst, a):
        rec("Y", [lambda: g.sync.dma_start(dst, a[0])], [a], [], 3.0, name)

    locs = [0]
    trip = lambda s: (None, [("~" + s, 0, 1, True)], 0)

    def remote(dst, name, lo, hi, a, rsem):
        rid, pid = topo.addr(dst)[:2]
        en = topo.engines(core, dst)[:4]
        locs[0] += len(en)
        rec("G", [lambda: g.remote_dma(T[name][:, lo:hi], a[0], T.sem[rsem], T.sem.loc, pid, rid, sum(1 << x for x in en))], [a], [trip(rsem)], 14.0, "remote")
        return len(en)

    lab = v("lab")
    load("Y", "ldla", v("lab", 0, 8), T.la)
    load("Y", "ldlb", v("lab", 8, 16), T.lb)
    load("Y", "ldco", v("cot", 0, 2560), T.co)
    load("S", "lddl", v("dls", 0, 128), T.dl)
    load("S", "ldx", v("X", 0, 2560), T.x0)
    load("Y", "ldth", (T.thi[0:8, 0:1], [("thi", 0, 1, True)], 1), T.th)
    load("Y", "ldwt", v("wtc"), T.wt)
    load("Y", "ldsu", v("sut", 0, 2560), T.su, [v("cot", 0, 2560)])
    landed = {}
    for s in range(1, RO):
        dst = T.cores[(rank + s) % N]
        k = remote(dst, "dls", 128 * s, 128 * s + 128, v("dls", 0, 128), "dl%da" % s)
        landed["dl%da" % s], landed["ab%da" % s] = k, k
        note("dl%da" % s, k, [("dls", 128 * s, 128 * s + 128, True, True)])
        note("ab%da" % s, k, [("abt", 16 * s, 16 * s + 16, True, True)])

    def spread(t):
        for k in range(16):
            act(v("dx%d" % (t % 2), k, 2048, 16), v("dls", 128 * t, 128 * t + 128))

    spread(0)

    CF, at = {}, [0]

    def cf(k, n):
        CF[k] = (at[0], n)
        at[0] += n
        return v("cf", CF[k][0], CF[k][0] + n)

    C = lambda k, lo=0, hi=None: v("cf", CF[k][0] + lo, CF[k][0] + (CF[k][1] if hi is None else hi))
    SM = {"allow_small_or_imprecise_dtypes": True}
    iota(v("tmp"), [[1, 256]], 0, 0, **SM)
    iota(v("ci", 128, 129), [[0, 1]], 0, 1)
    iota(cf("kc", 128), [[0, 8], [1, 16]], 0, 0, **SM)
    iota(cf("c4", 128), [[1, 8], [0, 16]], 0, 0, **SM)
    iota(v("jr"), [[1, 192]], 0, 0, **SM)
    col = lambda n: v("tmp", 0, n)
    cp(v("abt", 0, 16), lab)
    ms(v("cot", 2560, CW), 0)
    ms(v("sut", 2560, CW), 0)
    P = lambda i: v("pc", i, i + 1)
    cp(P(0), v("ci", 128, 129))
    for d, s1, op in ((129, 4, A.arith_shift_right), (130, 15, A.bitwise_and), (131, 5, A.arith_shift_right), (132, 16, A.bitwise_and)):
        ts(v("ci", d, d + 1), v("ci", 128, 129), s1, op)
    for d, s in ((1, 129), (2, 130), (3, 131)):
        cp(P(d), v("ci", s, s + 1))
    ts(P(5), v("ci", 132, 133), 1.0 / 16, A.mult)
    ts(P(4), P(5), -1.0, A.mult, 1.0, A.add)
    ts(P(6), P(3), 4.0, A.add)
    tt(P(9), P(0), P(2), A.subtract)
    ts(P(10), P(9), 15.0, A.add)
    MB = {"B1": 0, "B16k": 144, "W": 288, "I16": 432, "E": 560, "I": 720, "nI": 848, "U": 976}
    for i, k in enumerate(("T", "O", "C")):
        for b in range(4):
            MB[k + str(b)] = 1488 + 128 * (4 * i + b)
    mb = lambda k, n=128: v("mb", MB[k], MB[k] + n)
    slide = lambda k, m: v("mb", MB[k] + 15 - m, MB[k] + 143 - m)
    MF = {"I": 0, "BO": 128, "ON": 256, "E8": 384, "SW00": 512, "SW01": 640, "SW10": 768, "SW11": 896}
    mf = lambda k: v("mf", MF[k], MF[k] + 128)
    ts(mb("B1", 144), col(144), P(10), A.is_equal)
    act(cf("k16", 128), C("kc"), scale=1.0 / 16)
    ts(cf("R1", 128), C("kc"), 0.0, A.is_equal, 32768.0, A.mult)
    ts(cf("R3", 128), C("kc"), 0.0, A.is_gt)
    ts(mf("I"), col(128), P(0), A.is_equal)
    for cpx in range(2):
        for gp in range(2):
            ts(P(11 + 2 * cpx + gp), P(0), 16.0 * (gp - cpx), A.add)
            ts(mf("SW%d%d" % (cpx, gp)), col(128), P(11 + 2 * cpx + gp), A.is_equal, P(4 + cpx), A.mult)
    act(mb("I"), mf("I"))
    act(mb("nI"), mf("I"), scale=-1.0)
    ts(mb("W", 144), mb("B1", 144), v("wtc"), A.mult)
    ts(mf("E8"), C("c4"), P(0), A.is_equal)
    th8 = v("th8", 0, 1, 1, (0, 8))
    cp(th8, v("thi", 0, 1, 1, (0, 8)))
    mms(v("pM", 0, 1), [(v("mf", MF["E8"], MF["E8"] + 128, 1, (0, 8)), th8)], f32=True)
    cp(v("thb"), v("pM", 0, 1))
    cp(v("thv"), v("thb"))
    ts(cf("R2", 128), C("kc"), 0.0, A.is_gt, 16777216.0, A.mult)
    act(cf("pc2", 128), C("kc"), F.Identity, bias=15360.0, scale=-1024.0)
    act(mb("B16k", 144), mb("B1", 144), scale=16384.0)
    ts(mf("BO"), C("c4"), P(1), A.is_equal)
    ms(mf("ON"), 1.0)
    ts(cf("M16", 16), C("kc", 0, 16), P(2), A.is_equal)
    ts(cf("lf", 8), col(8), 16.0, A.mult, P(2), A.add)
    ts(cf("cT", 8), C("lf"), 2560.0, A.add)
    ts(cf("c15", 8), C("lf"), 16.0, A.mult, 15.0, A.add)
    ts(cf("hl", 8), C("lf"), 0.5, A.mult)
    ts(cf("c2", 8), C("lf"), -0.5, A.mult, 0.5, A.add)
    act(mb("I16"), mf("I"), scale=16.0)
    ts(v("ks"), C("kc"), P(2), A.is_lt, -1.0, A.mult)
    ts(P(18), P(3), 16.0, A.mult, P(2), A.add)
    ts(P(19), P(18), 64.0, A.add)
    for Q in range(2):
        for b in range(2):
            i = str(2 * Q + b)
            ts(mb("O" + i), C("c4"), P(6 if Q else 3), A.is_equal, P(4 + b), A.mult)
            ts(mb("C" + i), col(128), P(18 + Q), A.is_equal, P(4 + b), A.mult)
            tt(mb("T" + i), mb("O" + i), v("ks"), A.mult)
    ts(P(16), P(1), 32.0, A.mult, P(2), A.add)
    ts(P(17), P(16), 16.0, A.add)
    for b in range(2):
        ts(v("mb", MB["U"] + 256 * b, MB["U"] + 256 * b + 256), col(256), P(16 + b), A.is_equal)
    for Q in range(2):
        ts(v("k4", 48 * Q, 48 * Q + 48), col(48), 2.0, A.mult, float(Q), A.add)
        ts(v("mb", MB["E"] + 48 * Q, MB["E"] + 48 * Q + 48), v("k4", 48 * Q, 48 * Q + 48), P(0), A.is_equal)
    ms(v("P2", 96, 112), 4096.0)
    ms(cf("one", 96), 1.0)
    ts(cf("jl", 12), col(12), 16.0, A.mult, P(2), A.add)
    ts(cf("bj", 12), C("jl"), 0.5, A.add)
    ts(cf("jT", 12), C("jl"), 1536.0, A.add)
    for x, op in ((0, A.is_gt), (1536, A.is_equal)):
        ts(v("rr", x, x + 128), C("kc"), 0.0, op, 64.0, A.mult)
        for n, m in ((128, 128), (256, 256), (512, 512), (1024, 512)):
            act(v("rr", x + n, x + n + m), v("rr", x, x + m))

    ADD, SUB, MUL, MAX, MIN = A.add, A.subtract, A.mult, A.max, A.min
    X, cot, sut = v("X", 0, 2560), v("cot"), v("sut")
    PART = {0: (0, NA), 1: (NA, 128)}
    PU = {1: "pF", 0: "pM"}
    qv = lambda name, i, j=None: v(name, 512 * i, 512 * (i if j is None else j) + 512)

    def turn(src, nblk):
        o, i = v3("t3", 32, 0, nblk), v(src, 0, 32 * nblk)
        rec("V", [lambda: vec.transpose(o[0], i[0])], [i], [o], 32 * nblk * CY)

    def swap(nblk):
        for cpx in range(2):
            mms(v3("pQ", 32, 0, nblk, 16 * cpx, 16 * cpx + 16),
                [(mf("SW%d%d" % (cpx, gp)), v3("t3", 32, 0, nblk, 16 * gp, 16 * gp + 16)) for gp in range(2)], f32=True)

    def with_q(o, lo, hi, q0, b, op):
        tt(v(o, lo, hi), v3("pQ", 32, (q0 + lo) // 32, (q0 + hi) // 32), b, op)

    def distance(pd, w, buf, part):
        c0 = 4 * part
        mms(v(pd, 0, NA), [(slide(w, m), v3(buf, 256, c0, c0 + 4, 16 * m, 16 * m + 16)) for m in range(16)])

    def shifted(o, z, lists, dx, part, zs):
        qs = [i for i in (2 * part, 2 * part + 1) if i not in zs]
        for i in (2 * part, 2 * part + 1):
            if i in zs:
                act(qv(z, i), ind(X, v(lists, 32 * i, 32 * i + 32)))
                mms(v(BANK[i]), [(mb("I"), qv(z, i)), (mb("I"), qv(dx, i))])
                ts(qv(o, i), v(BANK[i]), 0.0, MAX, 63.0, MIN)
        if qs:
            i, j = qs[0], qs[-1]
            tt(qv(z, i, j), ind(X, v(lists, 32 * i, 32 * j + 32)), qv(dx, i, j), ADD)
            ts(qv(o, i, j), qv(z, i, j), 0.0, MAX, 63.0, MIN)

    def apart(xb, db, eb, ab, lists, l0, quarters):
        for i in quarters:
            act(qv(xb, i), ind(X, v(lists, l0 + 32 * i, l0 + 32 * i + 32)))
        for i in quarters:
            mms(v(BANK[i]), [(mb("I"), qv(xb, i)), (mb("nI"), qv(eb, i))])
            act(v3(ab, 256, 2 * i, 2 * i + 2), v(BANK[i]), F.Abs)
        for i in (3, 2, 0, 1):
            if i not in quarters:
                tt(qv(db, i), ind(X, v(lists, l0 + 32 * i, l0 + 32 * i + 32)), qv(eb, i), SUB)
                act(v3(ab, 256, 2 * i, 2 * i + 2), qv(db, i), F.Abs)

    for t in range(RO):
        dx = "dx%d" % (t % 2)
        last = t == RO - 1
        ab, here = v("abt", 16 * t, 16 * t + 16), [trip("ab%da" % t)]
        cp(v("dfk"), ind(cot, ab), here)
        for part in (1, 0):
            shifted("e1", "z", "dfk", dx, part, ZS1)
        cp(v("f2"), v("dfk"))
        turn("f2", 8)
        apart("xf", "da", "e1", "a3", "dfk", 128, FAR1)
        swap(8)
        distance("pD1", "B1", "a3", 1)
        distance("pD0", "B1", "a3", 0)
        for part in (1, 0):
            lo, hi = PART[part]
            tt(v("key", lo, hi), v("pD%d" % part, 0, NA), C("k16", lo, hi), ADD)
            scan(v("sc", lo, hi), C("R1", lo, hi), v("key", lo, hi), MAX, MIN)
            for c in range(lo // 16, hi // 16):
                ts(v("oh", 16 * c, 16 * c + 16), v("key", 16 * c, 16 * c + 16), v("sc", 16 * c + 15, 16 * c + 16), A.is_equal)
            with_q("pr", lo, hi, 0, v("oh", lo, hi), MUL)
            scan(v("ds", lo, hi), C("R3", lo, hi), v("pr", lo, hi), MUL, ADD)
            cp(v("d16", 4 * part, 4 * part + 4), v("ds", lo + 15, hi, 16))
            cp(v("sj", lo, hi), ind(sut, v("d16", 4 * part, 4 * part + 4)))
            shifted("e", "z2", "sj", dx, part, ZS2)
            mms(v(PU[part], 0, NA), [(slide("W", j), v("e", 16 * lo + j, 16 * hi, 16)) for j in range(16)])
            r = lambda k: v(k, lo, hi)
            cp(r("ui"), v(PU[part], 0, NA))
            ts(r("uv"), r("ui"), 4095, A.bitwise_and)
            ts(r("w1"), r("uv"), -2048.0, ADD)
            ts(r("w2"), r("uv"), 3232.0, ADD)
            tt(r("nn"), r("w1"), r("w2"), MUL)
            ts(r("ni"), r("nn"), 5, A.arith_shift_right, 1023, A.bitwise_and)
            cp(r("n16"), r("ni"))
            cp(r("nf"), r("ni"))
        with_q("prf", 0, 128, 128, v("oh"), MUL)
        scan(v("fs"), C("R3"), v("prf"), MUL, ADD)
        ts(v("al"), v("sc", 15, 128, 16), v("thv"), A.is_lt)
        tt(v("alT"), v("al"), C("cT"), MUL)
        apart("xn", "db", "e", "b3", "n16", 0, FAR2)
        turn("nf", 4)
        swap(4)
        distance("pD1", "B16k", "b3", 1)
        distance("pD0", "B16k", "b3", 0)
        with_q("pay", 0, 128, 0, C("pc2"), ADD)
        for part in (1, 0):
            lo, hi = PART[part]
            tt(v("key2", lo, hi), v("pD%d" % part, 0, NA), v("pay", lo, hi), ADD)
            scan(v("sc2", lo, hi), C("R2", lo, hi), v("key2", lo, hi), MIN, MAX)
        cp(v("af"), ab, here)
        tt(v("u8", 0, 8), v("ds", 15, 128, 16), v("af", 0, 8), SUB)
        tt(v("u8", 8, 16), v("fs", 15, 128, 16), v("af", 8, 16), SUB)
        for h in (0, 8):
            tt(v("u8", h, h + 8), v("u8", h, h + 8), v("al"), MUL)
        tt(v("abf"), v("u8"), v("af"), ADD)
        if not last:
            cp(v("abo", 16 * t, 16 * t + 16), v("abf"))
            remote(T.cores[(rank + 1) % N], "abt", 16 * t + 16, 16 * t + 32, v("abo", 16 * t, 16 * t + 16), "ab%da" % (t + 1))
            total(v("cnt"), v("al"))
        else:
            store("sta", T.ya[:], v("abf", 0, 8))
            store("stb", T.yb[:], v("abf", 8, 16))
        cp(v("k8"), v("sc2", 15, 128, 16))
        ts(v("n8"), v("k8"), 1023, A.bitwise_and)
        ts(v("j8"), v("k8"), 10, A.arith_shift_right, 15, A.bitwise_and)
        tt(v("nm"), v("n8"), v("alT"), MAX)
        cp(v("nl"), v("nm"))
        cp(v("cg"), ind(cot, v("nl")))
        rec("P", [lambda: ten.transpose(T.pX2[:, 0:128], T.cg[:, 0:128], mf("I")[0])], [v("cg"), mf("I")], [v("pX2", 0, 128)], 512 * PCY)
        ts(v("m128"), v("nm"), 128.0, MUL)
        tt(v("q"), v("m128"), C("lf"), ADD)
        tt(v("nb"), C("c2"), v("m128"), SUB)
        for c in range(8):
            act(v("nlx", 16 * c, 16 * c + 16), C("M16"), F.Copy, scale=v("q", c, c + 1))
        mms(v("pM", 0, 128), [(mf("BO"), v("nlx"))], f32=True)
        for c in range(8):
            act(v("ab1", 128 * c, 128 * c + 16 * c + 16), v("pM", 0, 16 * c + 16), F.Abs, bias=v("nb", c, c + 1))
        for c in range(8):
            act(v("rl", 128 * c, 128 * c + 16 * c + 16), v("ab1", 128 * c, 128 * c + 16 * c + 16), F.Relu, bias=C("hl", c, c + 1), scale=-1.0, acc=v("los", c, c + 1))
        ts(v("lt"), v("los"), 0.0, A.is_gt)
        tt(v("lt"), v("lt"), C("cT"), MUL)
        tt(v("tg"), v("lt"), v("nm"), MAX)
        cp(v("tg16"), v("tg"))
        tt(v("jf"), C("c15"), v("j8"), SUB)
        cp(v("jl"), v("jf"))
        cp(v("esel"), ind(v("e"), v("jl")))
        scatter(v("X"), v("tg16"), v("esel"))
        if last:
            store("stx0", T.yx[:, 0:1024], v("X", 0, 1024))
        ts(v("hi"), v("pX2", 0, 128), 1.0 / 32, MUL, 128.0 - 31.0 / 64, ADD)
        ts(v("hs"), v("hi"), -32.0, MUL, 4096.0, ADD)
        tt(v("lo"), v("pX2", 0, 128), v("hs"), ADD)
        for h in range(48 - NS, 48):
            act(v("sh", 128 * (h - 48 + NS), 128 * (h - 47 + NS)), v("hi"), F.Abs, bias=-160.0 - h)
        for h in range(48 - NS, 48):
            act(v("ohh", 128 * h, 128 * h + 128), v("sh", 128 * (h - 48 + NS), 128 * (h - 47 + NS)), F.Relu, bias=1.0, scale=-1.0)
        for h in range(48 - NS):
            ts(v("ohh", 128 * h, 128 * h + 128), v("hi"), 160.0 + h, A.is_equal)
        for h in range(32):
            ts(v("ohl", 128 * h, 128 * h + 128), v("lo"), float(h), A.is_equal)
        for pr in range(4):
            o, fq = v(("pF", "pX0", "pX1", "pD0")[pr], 0, 64, 1, (0, 96)), v("Fq", 64 * pr, 64 * pr + 64, 1, (0, 96))
            mms(o, [(v("ohh", 16 * pr + k, 6144, 64), v("ohl", 16 * pr + k, 4096, 64)) for k in range(16)])
            ts(fq, o, 0.0, A.is_gt)
        for gi in (0, 4, 1, 5, 2, 6, 3, 7):
            Q, q4 = divmod(gi, 4)
            pairs = [(v("Fq", 64 * q4 + Q, 64 * q4 + 64, 2, (0, 96)), v("mb", MB["E"] + 48 * Q, MB["E"] + 48 * Q + 48, 1, (0, 96)))]
            if t:
                pairs = [(v("mb", MB["U"] + 256 * b + 32 * gi, MB["U"] + 256 * b + 32 * gi + 32), v("old", b, 96, 2)) for b in range(2)] + pairs
            mms(v("pD1", 48 * Q, 48 * Q + 48, 1, (32 * q4, 32 * q4 + 32)), pairs)
        if not last:
            spread(t + 1)
            mms(v("pM", 0, 1), [(mf("ON"), v("cnt"))], f32=True)
            ts(v("ai"), v("pM", 0, 1), -1.0, MUL, 1024.0, ADD)
            ts(v("ai"), v("ai"), 63, A.bitwise_and)
            tt(v("thv"), v("thb"), v("ai"), ADD)
        ts(v("Fl"), v("pD1", 0, 96), 0.0, A.is_gt)
        for mi, bank in (("O", "pX0"), ("T", "pX1")) + ((("C", "pD0"),) if not last else ()):
            for b in range(2):
                mms(v(bank, b, 96, 2), [(mb(mi + str(2 * Q + b)), v("Fl", 48 * Q, 48 * Q + 48)) for Q in range(2)])
        scan(v("Sx"), C("one"), v("pX0", 0, 96), MUL, ADD)
        for c in range(12 - NV, 12):
            ts(v("sg", 96 * c, 96 * c + 96), v("Sx"), C("bj", c, c + 1), A.is_lt)
            total(v("xa", c, c + 1), v("sg", 96 * c, 96 * c + 96))
        for c in range(12 - NV):
            act(v("sg", 96 * c, 96 * c + 96), v("Sx"), F.Sign, bias=C("bj", c, c + 1), scale=-1.0, acc=v("xa", c, c + 1))
        tt(v("P2", 0, 96), v("Sx"), v("pX1", 0, 96), ADD)
        for x in ("xl", "xb"):
            ts(v(x, 0, 12 - NV), v("xa", 0, 12 - NV), 0.5, MUL, 48.0, ADD)
            cp(v(x, 12 - NV, 12), v("xa", 12 - NV, 12))
        tt(v("cm"), ind(v("P2"), v("xl")), v("jr"), A.is_le)
        mms(v("pD1", 0, 12), [(mb("I16"), v("xb"))] + [(slide("B1", m), v("cm", m, 192, 16)) for m in range(16)])
        ts(v("no16"), v("pD1", 0, 12), 1024.0, ADD)
        cp(v("s4"), ind(sut, v("no16")))
        cut = [sum(RC[:i]) for i in range(len(RC) + 1)]
        for lo, hi in zip(cut[1:], cut[2:]):
            act(v("R", 16 * lo, 16 * hi), ind(X, v("s4", lo, hi)))
        cp(v("R", 0, 16 * cut[1]), ind(X, v("s4", 0, cut[1])))
        ts(v("iv"), C("jl"), v("Sx", 95, 96), A.is_ge)
        tt(v("iv"), v("iv"), C("jT"), MUL)
        tt(v("vl"), v("pD1", 0, 12), v("iv"), MAX)
        cp(v("vl16"), v("vl"))
        if not last:
            ts(v("g2"), v("P2", 0, 96), 192.0, A.is_gt)
            tt(v("old"), v("pD0", 0, 96), v("g2"), MUL)
        for lo, hi in zip(cut, cut[1:]):
            n, r = 16 * (hi - lo), v("R", 16 * lo, 16 * hi)
            scan(v("mx", 16 * lo, 16 * hi), v("rr", 0, n), r, MIN, MAX)
            scan(v("mn", 16 * lo, 16 * hi), v("rr", 1536, 1536 + n), r, MAX, MIN)
            tt(v("sm", lo, hi), v("mx", 16 * lo + 15, 16 * hi, 16), v("mn", 16 * lo + 15, 16 * hi, 16), ADD)
            ts(v("vi", lo, hi), v("sm", lo, hi), 0.5, MUL, -0.25, ADD)
        scatter(v("X", 1024, XW), v("vl16"), v("vi"))
    store("stx1", T.yx[:, 1024:2560], v("X", 1024, 2560))
    flush()

    for e in ("V", "S", "P", "G"):
        wait("G", {e: cnt[e]})
    for k in LOADS:
        wait("G", {k: 16})
    for k in STORES:
        g.sync.wait_ge(T.sem[k], 16)
    g.wait_ge(T.sem.loc, locs[0])
    wait("G", landed)
